import numpy as np
import ml_dtypes


def mxq(x, axis, fmt="e4m3"):
    dtype, down = {"e4m3": (ml_dtypes.float8_e4m3fn, 7), "e5m2": (ml_dtypes.float8_e5m2, 14)}[fmt]
    v = np.moveaxis(np.asarray(x, np.float32).astype(ml_dtypes.bfloat16).astype(np.float64), axis, -1)
    blocks = v.reshape(v.shape[:-1] + (-1, 32))
    amax = np.abs(blocks).max(-1, keepdims=True)
    byte = np.maximum(np.where(amax > 0, np.frexp(amax)[1] - 1 + 127, 0) - down, 1)
    scale = np.exp2(byte - 127.0)
    codes = (blocks / scale).astype(np.float32).astype(dtype).astype(np.float64)
    return np.moveaxis((codes * scale).reshape(v.shape), -1, axis)


WIDE = False


def mx_kscale(k):
    if not WIDE:
        return np.ones(k)
    levels = np.array([10, -10, 5, -5, 0])
    if k % 512:
        return np.exp2(np.random.permutation(np.resize(levels, k // 32))).repeat(32)
    a = np.empty((k // 512, 16))
    for p in range(k // 512):
        a[p, :8] = np.random.permutation(np.resize(levels, 8))
        for g in range(8):
            far = levels[np.abs(levels - a[p, g]) >= 10]
            a[p, g + 8] = far[np.random.randint(len(far))]
    return np.exp2(a.ravel()).repeat(32)


def f64(x):
    return np.asarray(x).astype(np.float64)


def striped(idx):
    return np.tile(idx.reshape(-1, 16).T, (8, 1)).astype(np.uint16)


def unstriped(offs):
    return offs[:16].T.reshape(-1).astype(np.int64)


E2M1 = np.array([0.0, 0.5, 1.0, 1.5, 2.0, 3.0, 4.0, 6.0, -0.0, -0.5, -1.0, -1.5, -2.0, -3.0, -4.0, -6.0])


def pack_weight(w, fmt):
    k, n = w.shape
    w = f64(np.asarray(w, np.float32).astype(ml_dtypes.bfloat16)).reshape(k // 32, 32, n)
    amax = np.abs(w).max(1)
    if fmt == "e4m3":
        byte = np.frexp(amax)[1] - 1 + 127 - 7
    else:
        mant, ex = np.frexp(amax / 6.0)
        byte = np.where(mant > 0.5, ex, ex - 1) + 127
    byte = np.clip(np.where(amax > 0, byte, 1), 1, 254)
    scaled = (w * np.exp2(127.0 - byte)[:, None, :]).reshape(k, n).astype(np.float32)
    by_word = np.ascontiguousarray(scaled.reshape(k // 512, 128, 4, n).transpose(0, 1, 3, 2))
    if fmt == "e4m3":
        words = by_word.astype(ml_dtypes.float8_e4m3fn).view(np.uint8)
    else:
        c = by_word.astype(ml_dtypes.float4_e2m1fn).view(np.uint8) & 0xF
        words = (c[..., 0::2] | (c[..., 1::2] << 4)).reshape(k // 512, 128, 2 * n)
    return np.ascontiguousarray(words), np.ascontiguousarray(byte.astype(np.uint8).reshape(k // 512, 16, n))


def unpack_weight(words, scales, fmt):
    g, _, n = scales.shape
    words = np.ascontiguousarray(words).reshape(g, 128, n, -1)
    if fmt == "e4m3":
        vals = words.view(ml_dtypes.float8_e4m3fn).astype(np.float64)
    else:
        nib = np.empty((g, 128, n, 4), np.uint8)
        nib[..., 0::2] = words & 0xF
        nib[..., 1::2] = words >> 4
        vals = E2M1[nib]
    vals = vals * np.repeat(np.exp2(scales.astype(np.float64) - 127.0), 8, axis=1)[..., None]
    return vals.transpose(0, 1, 3, 2).reshape(g * 512, n)


def gelu(v):
    return 0.5 * v * (1.0 + np.tanh(np.sqrt(2.0 / np.pi) * (v + 0.044715 * v**3)))


K, K2, H, N, T, S = 1024, 512, 1024, 384, 2048, 1024

def setup_inputs():
    n = np.random.standard_normal
    s, s2, u = mx_kscale(K)[:, None], mx_kscale(K2)[:, None], mx_kscale(H)[:, None]
    tab_words, tab_scales = pack_weight(n((K, T)) * s, "e4m3")
    tab2_words, tab2_scales = pack_weight(n((K2, T)) * s2, "e4m3")
    b4_words, b4_scales = pack_weight(n((K2, H)) / np.sqrt(K2) / s2, "e2m1")
    return {
        "tab_words": tab_words, "tab_scales": tab_scales,
        "tab2_words": tab2_words, "tab2_scales": tab2_scales,
        "offs": striped(np.random.permutation(T)[:S]),
        "offs2": striped(np.random.permutation(T)[:S]),
        "a": (n((K, H)) / np.sqrt(K) / s).astype(np.float32),
        "b4_words": b4_words, "b4_scales": b4_scales,
        "gT": (np.exp(0.3 * n((H, T))) * u).astype(np.float32),
        "w": (2.0 * n((H, N)) / np.sqrt(H) / u).astype(np.float32),
    }

def reference(tab_words, tab_scales, tab2_words, tab2_scales, offs, offs2, a, b4_words, b4_scales, gT, w):
    v = unpack_weight(tab_words, tab_scales, "e4m3")[:, unstriped(offs)]
    v2 = unpack_weight(tab2_words, tab2_scales, "e4m3")[:, unstriped(offs2)]
    b = unpack_weight(b4_words, b4_scales, "e2m1")
    g = f64(gT)[:, unstriped(offs)]
    d = (mxq(f64(a), 0, "e4m3").T @ v) - (b.T @ v2)
    h = g * d / (1.0 + d * d)
    return mxq(f64(w), 0, "e4m3").T @ mxq(h, 0, "e4m3")

@@ -1,0 +1,360 @@
+from contextlib import ExitStack
+
+import concourse.mybir as mybir
+
+K, K2, H, N, T, S = 1024, 512, 1024, 384, 2048, 1024
+FLOPS = 2 * S * (K * H + K2 * H + H * N)
+
+F32 = mybir.dt.float32
+BF16 = mybir.dt.bfloat16
+I32 = mybir.dt.int32
+U32 = mybir.dt.uint32
+U16 = mybir.dt.uint16
+U8 = mybir.dt.uint8
+FP8X4 = mybir.dt.float8_e4m3fn_x4
+FP4X4 = mybir.dt.float4_e2m1fn_x4
+ACT = mybir.ActivationFunctionType
+MULT = mybir.AluOpType.mult
+
+P = 128
+PACK = 4
+KP = P * PACK
+CHUNKS = [128,128,256,256,256]
+STARTS = [sum(CHUNKS[:i]) for i in range(len(CHUNKS))]
+CH = 256
+BK = 128
+
+
+def tile_list_mesh_contact_forces_kernel(
+    tc, tab_words, tab_scales, tab2_words, tab2_scales, offs, offs2, a, b4_words, b4_scales, gT, w, out
+):
+    nc = tc.nc
+    with ExitStack() as ctx:
+        keep = ctx.enter_context(tc.tile_pool(name="keep", bufs=1))
+        ring = ctx.enter_context(tc.tile_pool(name="ring", bufs=2))
+        psum = ctx.enter_context(tc.psum_pool(name="psum", bufs=1))
+
+        def held(shape, dtype, name):
+            return keep.tile(shape, dtype, name=name, align_bytes=64)
+
+        lst = keep.tile([P, S // 16], U16, name="lst")
+        lst2 = keep.tile([P, S // 16], U16, name="lst2")
+        tw = [held([P, T], I32, "tw%d" % i) for i in range(3)]
+        ts = held([P, T], U8, "ts")
+        ts2 = held([P, T], U8, "ts2")
+        bw_raw = held([P, 2 * H], U8, "bw_raw")
+        bs_raw = held([P, H], U8, "bs_raw")
+        bw = held([P, 2 * H], U8, "bw")
+        bs = held([P, H], U8, "bs")
+        vw = [held([P, S], U32, "vw%d" % i) for i in range(3)]
+        vs = held([P, S], U8, "vs")
+        vs2 = held([P, S], U8, "vs2")
+        ac = [held([P, H], U32, "ac%d" % i) for i in range(2)]
+        asc = [held([P, H], U8, "asc%d" % i) for i in range(2)]
+        g = [held([P, T], F32, "g%d" % i) for i in range(8)]
+        w_raw = held([P, 2, PACK, N], F32, "w_raw")
+        w_bf = held([P, 2 * N * PACK], BF16, "w_bf")
+        wc = held([P, 2 * N], U32, "wc")
+        wsc = held([P, 2 * N], U8, "wsc")
+        hc = [held([P, S], U32, "hc%d" % i) for i in range(2)]
+        hsc = [held([P, S], U8, "hsc%d" % i) for i in range(2)]
+        one = held([P, 1], F32, "one")
+        warm = held([P, 1], F32, "warm")
+
+        nc.vector.memset(one[:], 1.0)
+        nc.scalar.activation(out=warm[:], in_=one[:], func=ACT.Abs_reciprocal_sqrt, bias=one[:])
+        for plane in (ts, ts2, bs_raw):
+            nc.vector.memset(plane[:].bitcast(I32), 0)
+
+        def load_words(i):
+            src = tab_words[i] if i < 2 else tab2_words[0]
+            nc.sync.dma_start(out=tw[i][:], in_=src.rearrange("p t i -> p (t i)").bitcast(I32))
+
+        def load_scales(plane, src):
+            rows = 4 * src.shape[0]
+            for q in range(4):
+                nc.sync.dma_start(
+                    out=plane[32 * q : 32 * q + rows, :].bitcast(I32),
+                    in_=src[:, 4 * q : 4 * q + 4, :].bitcast(I32) if rows > 4 else src[0, 4 * q : 4 * q + 4, :].bitcast(I32),
+                )
+
+        a_raw = {}
+
+        def load_a(kp, b):
+            t = ring.tile([P, PACK, KP], F32, name="a_raw", bufs=3)
+            a_raw[kp, b] = t
+            nc.sync.dma_start(
+                out=t[:], in_=a[kp * KP : (kp + 1) * KP, b * KP : (b + 1) * KP].rearrange("(p j) c -> p j c", j=PACK)
+            )
+
+        g_src = gT.rearrange("(b p t) n -> b t p n", p=P, t=PACK)
+
+        def load_g(b, t):
+            nc.sync.dma_start(out=g[4 * b + t][:], in_=g_src[b, t])
+
+        def load_w(b):
+            nc.sync.dma_start(out=w_raw[:, b], in_=w[b * KP : (b + 1) * KP, :].rearrange("(p j) n -> p j n", j=PACK))
+
+        a_bf = {}
+
+        def cast_a(kp, b, eng):
+            t = ring.tile([P, PACK, P, PACK], BF16, name="a_bf", bufs=2, align_bytes=64)
+            a_bf[kp, b] = t
+            dst = t[:].rearrange("p t m j -> p m j t")
+            src = a_raw[kp, b][:].rearrange("p j (m t) -> p m j t", t=PACK)
+            if eng == "S":
+                nc.scalar.activation(out=dst, in_=src, func=ACT.Copy, scale=-1.0)
+            else:
+                nc.vector.tensor_scalar(out=dst, in0=src, scalar1=-1.0, scalar2=None, op0=MULT)
+
+        def quant_a(kp, b):
+            cols = slice(b * KP, (b + 1) * KP)
+            nc.vector.quantize_mx(
+                out=ac[kp][:, cols].bitcast(FP8X4),
+                scales=asc[kp][:, cols],
+                in_=a_bf[kp, b][:].rearrange("p t m j -> p (t m j)"),
+            )
+
+        def cast_w(b):
+            nc.scalar.activation(
+                out=w_bf[:, b * N * PACK : (b + 1) * N * PACK].rearrange("p (c i j) -> p c j i", i=4, j=PACK),
+                in_=w_raw[:, b].rearrange("p j (c i) -> p c j i", i=4),
+                func=ACT.Copy,
+                scale=-1.0,
+            )
+
+        def quant_w():
+            for c0, c1 in ((0, 512), (512, 768)):
+                nc.vector.quantize_mx(
+                    out=wc[:, c0:c1].bitcast(FP8X4), scales=wsc[:, c0:c1], in_=w_bf[:, PACK * c0 : PACK * c1]
+                )
+
+        def gather(dst, window, offsets, n0, n1):
+            nc.vector.tensor_copy(out=dst[:, n0:n1], in_=window.indirect(offsets[:, n0 // 16 : n1 // 16]))
+
+        banks = {}
+        r_of = {}
+        h_of = {}
+
+        def displacement(u):
+            b, ch = divmod(u, len(CHUNKS))
+            n_lo, width = STARTS[ch], CHUNKS[ch]
+            s = ring.tile([P, PACK, width], F32, name="s", bufs=2)
+            for hb in range(width // BK):
+                bank = psum.tile([P, PACK, BK], F32, name="d_bank", bufs=6)
+                banks[u, hb] = bank
+                n0 = n_lo + hb * BK
+                cols = slice(n0, n0 + BK)
+                for t in range(PACK):
+                    m0 = b * KP + t * P
+                    rows = slice(m0, m0 + P)
+                    for kp in range(2):
+                        nc.tensor.matmul_mx(
+                            out=bank[:, t, :],
+                            lhsT=ac[kp][:, rows].bitcast(FP8X4),
+                            lhsT_scale=asc[kp][:, rows],
+                            rhs=vw[kp][:, cols].bitcast(FP8X4),
+                            rhs_scale=vs[4 * kp :, cols],
+                            start=(kp == 0),
+                            stop=False,
+                        )
+                    nc.tensor.matmul_mx(
+                        out=bank[:, t, :],
+                        lhsT=bw[:, 2 * m0 : 2 * (m0 + P)].bitcast(FP4X4),
+                        lhsT_scale=bs[:, rows],
+                        rhs=vw[2][:, cols].bitcast(FP8X4),
+                        rhs_scale=vs2[:, cols],
+                        start=False,
+                        stop=True,
+                    )
+                nc.scalar.activation(out=s[:, :, hb * BK : (hb + 1) * BK], in_=bank[:], func=ACT.Square)
+            nc.scalar.activation(out=s[:], in_=s[:], func=ACT.Abs_reciprocal_sqrt, bias=one[:])
+            r = ring.tile([P, PACK, width], F32, name="r", bufs=3)
+            r_of[u] = r
+            nc.scalar.activation(out=r[:], in_=s[:], func=ACT.Square)
+
+        u_of = {}
+
+        def stiffness(u, t):
+            b, ch = divmod(u, len(CHUNKS))
+            n_lo, width = STARTS[ch], CHUNKS[ch]
+            if u not in u_of:
+                u_of[u] = ring.tile([P, PACK, width], F32, name="gr", bufs=2)
+            nc.vector.tensor_tensor(
+                out=u_of[u][:, t, :],
+                in0=g[4 * b + t][:].indirect(lst[:, n_lo // 16 : (n_lo + width) // 16]),
+                in1=r_of[u][:, t, :],
+                op=MULT,
+            )
+
+        def response(u):
+            width = CHUNKS[u % len(CHUNKS)]
+            hb16 = ring.tile([P, width, PACK], BF16, name="h_bf", bufs=2, align_bytes=64)
+            h_of[u] = hb16
+            for hb in range(width // BK):
+                cols = slice(hb * BK, (hb + 1) * BK)
+                nc.vector.tensor_tensor(
+                    out=hb16[:, cols, :].rearrange("p (c i) t -> p c t i", i=4),
+                    in0=banks[u, hb][:].rearrange("p t (c i) -> p c t i", i=4),
+                    in1=u_of[u][:, :, cols].rearrange("p t (c i) -> p c t i", i=4),
+                    op=MULT,
+                )
+
+        def quant_h(u):
+            b, ch = divmod(u, len(CHUNKS))
+            n_lo, width = STARTS[ch], CHUNKS[ch]
+            cols = slice(n_lo, n_lo + width)
+            nc.vector.quantize_mx(
+                out=hc[b][:, cols].bitcast(FP8X4), scales=hsc[b][:, cols], in_=h_of[u][:].rearrange("p n t -> p (n t)")
+            )
+
+        out_v = out.rearrange("(c p) j -> p c j", p=P)
+
+        def forces(ch, how):
+            width = CHUNKS[ch]
+            cols = slice(STARTS[ch], STARTS[ch] + width)
+            stage = ring.tile([P, N // P, width], F32, name="stage", bufs=2)
+            for c in range(N // P):
+                acc = psum.tile([P, width], F32, name="o_bank", bufs=2)
+                for b in range(2):
+                    rows = slice(b * N + c * P, b * N + (c + 1) * P)
+                    nc.tensor.matmul_mx(
+                        out=acc[:],
+                        lhsT=wc[:, rows].bitcast(FP8X4),
+                        lhsT_scale=wsc[:, rows],
+                        rhs=hc[b][:, cols].bitcast(FP8X4),
+                        rhs_scale=hsc[b][:, cols],
+                        start=(b == 0),
+                        stop=(b == 1),
+                    )
+                if how[c] == "S":
+                    nc.scalar.copy(out=stage[:, c, :], in_=acc[:])
+                else:
+                    nc.vector.tensor_copy(out=stage[:, c, :], in_=acc[:])
+                if how[3] == "x":
+                    nc.sync.dma_start(out=out_v[:, c, cols], in_=stage[:, c, :])
+            if how[3] != "x":
+                nc.sync.dma_start(out=out_v[:, :, cols], in_=stage[:])
+
+        nc.sync.dma_start(lst[:], offs)
+        load_scales(ts, tab_scales)
+        nc.sync.dma_start(out=bw_raw[:].bitcast(I32), in_=b4_words[0].bitcast(I32))
+        load_words(0)
+        nc.sync.dma_start(lst2[:], offs2)
+        load_a(0, 0)
+        load_scales(ts2, tab2_scales)
+        load_words(1)
+        load_a(1, 0)
+        load_scales(bs_raw, b4_scales)
+        load_words(2)
+        load_g(0, 0)
+        load_g(0, 1)
+        load_g(0, 2)
+        load_g(0, 3)
+        load_a(0, 1)
+        load_a(1, 1)
+        load_g(1, 0)
+        load_g(1, 1)
+        load_w(0)
+        load_g(1, 2)
+        load_w(1)
+        load_g(1, 3)
+        gather(vs, ts[:], lst, 0, 1024)
+        gather(vw[0], tw[0][:].bitcast(U32), lst, 0, 1024)
+        cast_a(0, 0, "S")
+        nc.vector.tensor_copy(out=bw[:].bitcast(U16).rearrange("p (b t m) -> p b t m", b=2, t=PACK), in_=bw_raw[:].bitcast(U16).rearrange("p (b m t) -> p b t m", b=2, t=PACK))
+        gather(vs2, ts2[:], lst2, 0, 256)
+        gather(vw[1], tw[1][:].bitcast(U32), lst, 0, 256)
+        quant_a(0, 0)
+        cast_a(1, 0, "S")
+        nc.vector.tensor_copy(out=bs[:].rearrange("p (b t m) -> p b t m", b=2, t=PACK), in_=bs_raw[:].rearrange("p (b m t) -> p b t m", b=2, t=PACK))
+        quant_a(1, 0)
+        gather(vw[2], tw[2][:].bitcast(U32), lst2, 0, 256)
+        gather(vs2, ts2[:], lst2, 256, 512)
+        gather(vw[1], tw[1][:].bitcast(U32), lst, 256, 512)
+        gather(vw[2], tw[2][:].bitcast(U32), lst2, 256, 512)
+        gather(vs2, ts2[:], lst2, 512, 1024)
+        gather(vw[1], tw[1][:].bitcast(U32), lst, 512, 1024)
+        gather(vw[2], tw[2][:].bitcast(U32), lst2, 512, 1024)
+        displacement(0)
+        displacement(1)
+        displacement(2)
+        stiffness(0, 0)
+        stiffness(0, 1)
+        stiffness(0, 2)
+        stiffness(0, 3)
+        response(0)
+        displacement(3)
+        stiffness(1, 0)
+        quant_h(0)
+        stiffness(1, 1)
+        stiffness(1, 2)
+        stiffness(1, 3)
+        response(1)
+        displacement(4)
+        stiffness(2, 0)
+        quant_h(1)
+        stiffness(2, 1)
+        stiffness(2, 2)
+        stiffness(2, 3)
+        response(2)
+        cast_a(0, 1, "S")
+        quant_a(0, 1)
+        cast_a(1, 1, "V")
+        quant_a(1, 1)
+        displacement(7)
+        stiffness(3, 0)
+        quant_h(2)
+        stiffness(3, 1)
+        stiffness(3, 2)
+        stiffness(3, 3)
+        response(3)
+        displacement(8)
+        stiffness(4, 0)
+        quant_h(3)
+        stiffness(4, 1)
+        stiffness(4, 2)
+        stiffness(4, 3)
+        response(4)
+        cast_w(0)
+        cast_w(1)
+        quant_w()
+        displacement(9)
+        stiffness(7, 0)
+        quant_h(4)
+        stiffness(7, 1)
+        stiffness(7, 2)
+        stiffness(7, 3)
+        response(7)
+        displacement(5)
+        stiffness(8, 0)
+        quant_h(7)
+        forces(2, "SSSo")
+        stiffness(8, 1)
+        stiffness(8, 2)
+        stiffness(8, 3)
+        response(8)
+        displacement(6)
+        stiffness(9, 0)
+        quant_h(8)
+        forces(3, "SSSo")
+        stiffness(9, 1)
+        stiffness(9, 2)
+        stiffness(9, 3)
+        response(9)
+        stiffness(5, 0)
+        quant_h(9)
+        forces(4, "SSSo")
+        stiffness(5, 1)
+        stiffness(5, 2)
+        stiffness(5, 3)
+        response(5)
+        stiffness(6, 0)
+        quant_h(5)
+        forces(0, "SVSx")
+        stiffness(6, 1)
+        stiffness(6, 2)
+        stiffness(6, 3)
+        response(6)
+        quant_h(6)
+        forces(1, "SVSx")

@@ -19,9 +19,7 @@ MULT = mybir.AluOpType.mult
 P = 128
 PACK = 4
 KP = P * PACK
-CHUNKS = [128,128,256,256,256]
-STARTS = [sum(CHUNKS[:i]) for i in range(len(CHUNKS))]
-CH = 256
+UNITS = [[0,0,256],[0,256,256],[0,512,256],[0,768,256],[1,0,256],[1,256,256],[1,512,256],[1,768,256]]
 BK = 128
 
 
@@ -58,6 +56,7 @@ def tile_list_mesh_contact_forces_kernel(
         wsc = held([P, 2 * N], U8, "wsc")
         hc = [held([P, S], U32, "hc%d" % i) for i in range(2)]
         hsc = [held([P, S], U8, "hsc%d" % i) for i in range(2)]
+        gg = held([P, 2, S], F32, "gg")
         one = held([P, 1], F32, "one")
         warm = held([P, 1], F32, "warm")
 
@@ -115,13 +114,13 @@ def tile_list_mesh_contact_forces_kernel(
                 in_=a_bf[kp, b][:].rearrange("p t m j -> p (t m j)"),
             )
 
-        def cast_w(b):
-            nc.scalar.activation(
-                out=w_bf[:, b * N * PACK : (b + 1) * N * PACK].rearrange("p (c i j) -> p c j i", i=4, j=PACK),
-                in_=w_raw[:, b].rearrange("p j (c i) -> p c j i", i=4),
-                func=ACT.Copy,
-                scale=-1.0,
-            )
+        def cast_w(b, eng):
+            dst = w_bf[:, b * N * PACK : (b + 1) * N * PACK].rearrange("p (c i j) -> p c j i", i=4, j=PACK)
+            src = w_raw[:, b].rearrange("p j (c i) -> p c j i", i=4)
+            if eng == "S":
+                nc.scalar.activation(out=dst, in_=src, func=ACT.Copy, scale=-1.0)
+            else:
+                nc.vector.tensor_scalar(out=dst, in0=src, scalar1=-1.0, scalar2=None, op0=MULT)
 
         def quant_w():
             for c0, c1 in ((0, 512), (512, 768)):
@@ -135,13 +134,14 @@ def tile_list_mesh_contact_forces_kernel(
         banks = {}
         r_of = {}
         h_of = {}
+        u_of = {}
 
-        def displacement(u):
-            b, ch = divmod(u, len(CHUNKS))
-            n_lo, width = STARTS[ch], CHUNKS[ch]
-            s = ring.tile([P, PACK, width], F32, name="s", bufs=2)
+        def displacement(u, groups):
+            b, n_lo, width = UNITS[u]
+            r = ring.tile([P, PACK, width], F32, name="r", bufs=3)
+            r_of[u] = r
             for hb in range(width // BK):
-                bank = psum.tile([P, PACK, BK], F32, name="d_bank", bufs=6)
+                bank = psum.tile([P, PACK, BK], F32, name="bank", bufs=8)
                 banks[u, hb] = bank
                 n0 = n_lo + hb * BK
                 cols = slice(n0, n0 + BK)
@@ -167,17 +167,15 @@ def tile_list_mesh_contact_forces_kernel(
                         start=False,
                         stop=True,
                     )
-                nc.scalar.activation(out=s[:, :, hb * BK : (hb + 1) * BK], in_=bank[:], func=ACT.Square)
-            nc.scalar.activation(out=s[:], in_=s[:], func=ACT.Abs_reciprocal_sqrt, bias=one[:])
-            r = ring.tile([P, PACK, width], F32, name="r", bufs=3)
-            r_of[u] = r
-            nc.scalar.activation(out=r[:], in_=s[:], func=ACT.Square)
-
-        u_of = {}
+                nc.scalar.activation(out=r[:, :, hb * BK : (hb + 1) * BK], in_=bank[:], func=ACT.Square)
+            per = PACK // groups
+            for gi in range(groups):
+                part = r[:, gi * per : (gi + 1) * per, :]
+                nc.scalar.activation(out=part, in_=part, func=ACT.Abs_reciprocal_sqrt, bias=one[:])
+                nc.scalar.activation(out=part, in_=part, func=ACT.Square)
 
         def stiffness(u, t):
-            b, ch = divmod(u, len(CHUNKS))
-            n_lo, width = STARTS[ch], CHUNKS[ch]
+            b, n_lo, width = UNITS[u]
             if u not in u_of:
                 u_of[u] = ring.tile([P, PACK, width], F32, name="gr", bufs=2)
             nc.vector.tensor_tensor(
@@ -187,35 +185,42 @@ def tile_list_mesh_contact_forces_kernel(
                 op=MULT,
             )
 
-        def response(u):
-            width = CHUNKS[u % len(CHUNKS)]
-            hb16 = ring.tile([P, width, PACK], BF16, name="h_bf", bufs=2, align_bytes=64)
-            h_of[u] = hb16
-            for hb in range(width // BK):
-                cols = slice(hb * BK, (hb + 1) * BK)
-                nc.vector.tensor_tensor(
-                    out=hb16[:, cols, :].rearrange("p (c i) t -> p c t i", i=4),
-                    in0=banks[u, hb][:].rearrange("p t (c i) -> p c t i", i=4),
-                    in1=u_of[u][:, :, cols].rearrange("p t (c i) -> p c t i", i=4),
-                    op=MULT,
-                )
+        def stiffness_early(u):
+            b, n_lo, width = UNITS[u]
+            if u not in u_of:
+                u_of[u] = ring.tile([P, PACK, width], F32, name="gr", bufs=2)
+            nc.vector.tensor_tensor(
+                out=u_of[u][:, 0:2, :], in0=gg[:, :, n_lo : n_lo + width], in1=r_of[u][:, 0:2, :], op=MULT
+            )
 
-        def quant_h(u):
-            b, ch = divmod(u, len(CHUNKS))
-            n_lo, width = STARTS[ch], CHUNKS[ch]
-            cols = slice(n_lo, n_lo + width)
+        def response(u, hb):
+            width = UNITS[u][2]
+            if u not in h_of:
+                h_of[u] = ring.tile([P, width, PACK], BF16, name="h_bf", bufs=2, align_bytes=64)
+            cols = slice(hb * BK, (hb + 1) * BK)
+            nc.vector.tensor_tensor(
+                out=h_of[u][:, cols, :].rearrange("p (c i) t -> p c t i", i=4),
+                in0=banks[u, hb][:].rearrange("p t (c i) -> p c t i", i=4),
+                in1=u_of[u][:, :, cols].rearrange("p t (c i) -> p c t i", i=4),
+                op=MULT,
+            )
+
+        def quant_h(u, off, width):
+            b, n_lo = UNITS[u][:2]
+            cols = slice(n_lo + off, n_lo + off + width)
             nc.vector.quantize_mx(
-                out=hc[b][:, cols].bitcast(FP8X4), scales=hsc[b][:, cols], in_=h_of[u][:].rearrange("p n t -> p (n t)")
+                out=hc[b][:, cols].bitcast(FP8X4),
+                scales=hsc[b][:, cols],
+                in_=h_of[u][:, off : off + width, :].rearrange("p n t -> p (n t)"),
             )
 
         out_v = out.rearrange("(c p) j -> p c j", p=P)
 
-        def forces(ch, how):
-            width = CHUNKS[ch]
-            cols = slice(STARTS[ch], STARTS[ch] + width)
-            stage = ring.tile([P, N // P, width], F32, name="stage", bufs=2)
+        def forces(n_lo, width, how):
+            cols = slice(n_lo, n_lo + width)
+            stage = ring.tile([P, N // P, width], F32, name="stage", bufs=3)
             for c in range(N // P):
-                acc = psum.tile([P, width], F32, name="o_bank", bufs=2)
+                acc = psum.tile([P, width], F32, name="bank", bufs=8)
                 for b in range(2):
                     rows = slice(b * N + c * P, b * N + (c + 1) * P)
                     nc.tensor.matmul_mx(
@@ -236,125 +241,118 @@ def tile_list_mesh_contact_forces_kernel(
             if how[3] != "x":
                 nc.sync.dma_start(out=out_v[:, :, cols], in_=stage[:])
 
+        load_words(0)
         nc.sync.dma_start(lst[:], offs)
         load_scales(ts, tab_scales)
-        nc.sync.dma_start(out=bw_raw[:].bitcast(I32), in_=b4_words[0].bitcast(I32))
-        load_words(0)
-        nc.sync.dma_start(lst2[:], offs2)
         load_a(0, 0)
+        nc.sync.dma_start(out=bw_raw[:].bitcast(I32), in_=b4_words[0].bitcast(I32))
         load_scales(ts2, tab2_scales)
-        load_words(1)
         load_a(1, 0)
+        nc.sync.dma_start(lst2[:], offs2)
+        load_words(1)
         load_scales(bs_raw, b4_scales)
         load_words(2)
+        load_a(0, 1)
         load_g(0, 0)
         load_g(0, 1)
+        load_a(1, 1)
         load_g(0, 2)
         load_g(0, 3)
-        load_a(0, 1)
-        load_a(1, 1)
         load_g(1, 0)
         load_g(1, 1)
-        load_w(0)
         load_g(1, 2)
         load_w(1)
+        load_w(0)
         load_g(1, 3)
-        gather(vs, ts[:], lst, 0, 1024)
-        gather(vw[0], tw[0][:].bitcast(U32), lst, 0, 1024)
         cast_a(0, 0, "S")
+        cast_a(1, 0, "S")
         nc.vector.tensor_copy(out=bw[:].bitcast(U16).rearrange("p (b t m) -> p b t m", b=2, t=PACK), in_=bw_raw[:].bitcast(U16).rearrange("p (b m t) -> p b t m", b=2, t=PACK))
+        nc.vector.tensor_copy(out=bs[:].rearrange("p (b t m) -> p b t m", b=2, t=PACK), in_=bs_raw[:].rearrange("p (b m t) -> p b t m", b=2, t=PACK))
+        quant_a(0, 0)
+        quant_a(1, 0)
         gather(vs2, ts2[:], lst2, 0, 256)
         gather(vw[1], tw[1][:].bitcast(U32), lst, 0, 256)
-        quant_a(0, 0)
-        cast_a(1, 0, "S")
-        nc.vector.tensor_copy(out=bs[:].rearrange("p (b t m) -> p b t m", b=2, t=PACK), in_=bs_raw[:].rearrange("p (b m t) -> p b t m", b=2, t=PACK))
-        quant_a(1, 0)
         gather(vw[2], tw[2][:].bitcast(U32), lst2, 0, 256)
+        gather(vw[0], tw[0][:].bitcast(U32), lst, 0, 1024)
+        gather(vs, ts[:], lst, 0, 1024)
+        cast_a(0, 1, "S")
+        quant_a(0, 1)
+        displacement(0, 1)
         gather(vs2, ts2[:], lst2, 256, 512)
         gather(vw[1], tw[1][:].bitcast(U32), lst, 256, 512)
         gather(vw[2], tw[2][:].bitcast(U32), lst2, 256, 512)
         gather(vs2, ts2[:], lst2, 512, 1024)
         gather(vw[1], tw[1][:].bitcast(U32), lst, 512, 1024)
         gather(vw[2], tw[2][:].bitcast(U32), lst2, 512, 1024)
-        displacement(0)
-        displacement(1)
-        displacement(2)
-        stiffness(0, 0)
-        stiffness(0, 1)
-        stiffness(0, 2)
-        stiffness(0, 3)
-        response(0)
-        displacement(3)
-        stiffness(1, 0)
-        quant_h(0)
-        stiffness(1, 1)
-        stiffness(1, 2)
-        stiffness(1, 3)
-        response(1)
-        displacement(4)
-        stiffness(2, 0)
-        quant_h(1)
-        stiffness(2, 1)
-        stiffness(2, 2)
-        stiffness(2, 3)
-        response(2)
-        cast_a(0, 1, "S")
-        quant_a(0, 1)
+        gather(gg[:, 0, :], g[0][:], lst, 0, 1024)
+        gather(gg[:, 1, :], g[1][:], lst, 0, 1024)
+        displacement(1, 1)
         cast_a(1, 1, "V")
         quant_a(1, 1)
-        displacement(7)
-        stiffness(3, 0)
-        quant_h(2)
-        stiffness(3, 1)
+        displacement(2, 1)
+        stiffness_early(0)
+        stiffness(0, 2)
+        stiffness(0, 3)
+        response(0, 0)
+        response(0, 1)
+        displacement(3, 1)
+        stiffness_early(1)
+        quant_h(0, 0, 256)
+        stiffness(1, 2)
+        stiffness(1, 3)
+        response(1, 0)
+        response(1, 1)
+        displacement(4, 2)
+        stiffness_early(2)
+        quant_h(1, 0, 256)
+        stiffness(2, 2)
+        stiffness(2, 3)
+        response(2, 0)
+        response(2, 1)
+        displacement(5, 2)
+        stiffness_early(3)
+        quant_h(2, 0, 256)
         stiffness(3, 2)
         stiffness(3, 3)
-        response(3)
-        displacement(8)
+        response(3, 0)
+        response(3, 1)
+        cast_w(1, "S")
+        displacement(6, 2)
         stiffness(4, 0)
-        quant_h(3)
+        quant_h(3, 0, 256)
         stiffness(4, 1)
         stiffness(4, 2)
         stiffness(4, 3)
-        response(4)
-        cast_w(0)
-        cast_w(1)
+        response(4, 0)
+        response(4, 1)
+        cast_w(0, "S")
         quant_w()
-        displacement(9)
-        stiffness(7, 0)
-        quant_h(4)
-        stiffness(7, 1)
-        stiffness(7, 2)
-        stiffness(7, 3)
-        response(7)
-        displacement(5)
-        stiffness(8, 0)
-        quant_h(7)
-        forces(2, "SSSo")
-        stiffness(8, 1)
-        stiffness(8, 2)
-        stiffness(8, 3)
-        response(8)
-        displacement(6)
-        stiffness(9, 0)
-        quant_h(8)
-        forces(3, "SSSo")
-        stiffness(9, 1)
-        stiffness(9, 2)
-        stiffness(9, 3)
-        response(9)
+        displacement(7, 2)
         stiffness(5, 0)
-        quant_h(9)
-        forces(4, "SSSo")
+        quant_h(4, 0, 256)
+        forces(0, 256, "SSSx")
         stiffness(5, 1)
         stiffness(5, 2)
         stiffness(5, 3)
-        response(5)
+        response(5, 0)
+        response(5, 1)
         stiffness(6, 0)
-        quant_h(5)
-        forces(0, "SVSx")
+        quant_h(5, 0, 256)
+        forces(256, 256, "SSSx")
         stiffness(6, 1)
         stiffness(6, 2)
         stiffness(6, 3)
-        response(6)
-        quant_h(6)
-        forces(1, "SVSx")
+        response(6, 0)
+        response(6, 1)
+        stiffness(7, 0)
+        quant_h(6, 0, 256)
+        forces(512, 256, "SSSo")
+        stiffness(7, 1)
+        stiffness(7, 2)
+        stiffness(7, 3)
+        response(7, 0)
+        response(7, 1)
+        quant_h(7, 0, 128)
+        forces(768, 128, "SVVx")
+        quant_h(7, 128, 128)
+        forces(896, 128, "SVSx")

@@ -70,11 +70,13 @@ def tile_list_mesh_contact_forces_kernel(
             nc.sync.dma_start(out=tw[i][:], in_=src.rearrange("p t i -> p (t i)").bitcast(I32))
 
         def load_scales(plane, src):
-            rows = 4 * src.shape[0]
+            for r in range(4):
+                nc.sync.dma_start(out=plane[r:P:32, :].bitcast(I32), in_=src[0, r:16:4, :].bitcast(I32))
+
+        def load_table_scales():
             for q in range(4):
-                nc.sync.dma_start(
-                    out=plane[32 * q : 32 * q + rows, :].bitcast(I32),
-                    in_=src[:, 4 * q : 4 * q + 4, :].bitcast(I32) if rows > 4 else src[0, 4 * q : 4 * q + 4, :].bitcast(I32),
+                nc.gpsimd.dma_start(
+                    out=ts[32 * q + 4 : 32 * q + 12, :].bitcast(I32), in_=tab_scales[:, 4 * q : 4 * q + 4, :].bitcast(I32)
                 )
 
         a_raw = {}
@@ -154,7 +156,7 @@ def tile_list_mesh_contact_forces_kernel(
                             lhsT=ac[kp][:, rows].bitcast(FP8X4),
                             lhsT_scale=asc[kp][:, rows],
                             rhs=vw[kp][:, cols].bitcast(FP8X4),
-                            rhs_scale=vs[4 * kp :, cols],
+                            rhs_scale=vs[4 + 4 * kp :, cols],
                             start=(kp == 0),
                             stop=False,
                         )
@@ -241,61 +243,57 @@ def tile_list_mesh_contact_forces_kernel(
             if how[3] != "x":
                 nc.sync.dma_start(out=out_v[:, :, cols], in_=stage[:])
 
+        load_table_scales()
         load_words(0)
         nc.sync.dma_start(lst[:], offs)
-        load_scales(ts, tab_scales)
+        load_scales(bs_raw, b4_scales)
         load_a(0, 0)
         nc.sync.dma_start(out=bw_raw[:].bitcast(I32), in_=b4_words[0].bitcast(I32))
-        load_scales(ts2, tab2_scales)
-        load_a(1, 0)
-        nc.sync.dma_start(lst2[:], offs2)
         load_words(1)
-        load_scales(bs_raw, b4_scales)
+        load_scales(ts2, tab2_scales)
+        nc.sync.dma_start(lst2[:], offs2)
+        load_a(1, 0)
         load_words(2)
         load_a(0, 1)
         load_g(0, 0)
         load_g(0, 1)
-        load_a(1, 1)
         load_g(0, 2)
         load_g(0, 3)
+        load_a(1, 1)
+        load_w(0)
         load_g(1, 0)
         load_g(1, 1)
-        load_g(1, 2)
         load_w(1)
-        load_w(0)
+        load_g(1, 2)
         load_g(1, 3)
         cast_a(0, 0, "S")
         cast_a(1, 0, "S")
-        nc.vector.tensor_copy(out=bw[:].bitcast(U16).rearrange("p (b t m) -> p b t m", b=2, t=PACK), in_=bw_raw[:].bitcast(U16).rearrange("p (b m t) -> p b t m", b=2, t=PACK))
-        nc.vector.tensor_copy(out=bs[:].rearrange("p (b t m) -> p b t m", b=2, t=PACK), in_=bs_raw[:].rearrange("p (b m t) -> p b t m", b=2, t=PACK))
         quant_a(0, 0)
         quant_a(1, 0)
-        gather(vs2, ts2[:], lst2, 0, 256)
-        gather(vw[1], tw[1][:].bitcast(U32), lst, 0, 256)
-        gather(vw[2], tw[2][:].bitcast(U32), lst2, 0, 256)
         gather(vw[0], tw[0][:].bitcast(U32), lst, 0, 1024)
         gather(vs, ts[:], lst, 0, 1024)
-        cast_a(0, 1, "S")
-        quant_a(0, 1)
+        gather(vw[1], tw[1][:].bitcast(U32), lst, 0, 1024)
+        gather(vs2, ts2[:], lst2, 0, 1024)
+        gather(vw[2], tw[2][:].bitcast(U32), lst2, 0, 256)
+        nc.vector.tensor_copy(out=bw[:].bitcast(U16).rearrange("p (b t m) -> p b t m", b=2, t=PACK), in_=bw_raw[:].bitcast(U16).rearrange("p (b m t) -> p b t m", b=2, t=PACK))
+        nc.vector.tensor_copy(out=bs[:].rearrange("p (b t m) -> p b t m", b=2, t=PACK), in_=bs_raw[:].rearrange("p (b m t) -> p b t m", b=2, t=PACK))
+        cast_a(0, 1, "V")
         displacement(0, 1)
-        gather(vs2, ts2[:], lst2, 256, 512)
-        gather(vw[1], tw[1][:].bitcast(U32), lst, 256, 512)
         gather(vw[2], tw[2][:].bitcast(U32), lst2, 256, 512)
-        gather(vs2, ts2[:], lst2, 512, 1024)
-        gather(vw[1], tw[1][:].bitcast(U32), lst, 512, 1024)
         gather(vw[2], tw[2][:].bitcast(U32), lst2, 512, 1024)
+        quant_a(0, 1)
         gather(gg[:, 0, :], g[0][:], lst, 0, 1024)
         gather(gg[:, 1, :], g[1][:], lst, 0, 1024)
         displacement(1, 1)
-        cast_a(1, 1, "V")
-        quant_a(1, 1)
         displacement(2, 1)
         stiffness_early(0)
         stiffness(0, 2)
         stiffness(0, 3)
         response(0, 0)
         response(0, 1)
-        displacement(3, 1)
+        cast_a(1, 1, "V")
+        quant_a(1, 1)
+        displacement(3, 2)
         stiffness_early(1)
         quant_h(0, 0, 256)
         stiffness(1, 2)
@@ -316,6 +314,7 @@ def tile_list_mesh_contact_forces_kernel(
         stiffness(3, 3)
         response(3, 0)
         response(3, 1)
+        cast_w(0, "S")
         cast_w(1, "S")
         displacement(6, 2)
         stiffness(4, 0)
@@ -325,12 +324,11 @@ def tile_list_mesh_contact_forces_kernel(
         stiffness(4, 3)
         response(4, 0)
         response(4, 1)
-        cast_w(0, "S")
         quant_w()
         displacement(7, 2)
         stiffness(5, 0)
         quant_h(4, 0, 256)
-        forces(0, 256, "SSSx")
+        forces(0, 256, "SSSo")
         stiffness(5, 1)
         stiffness(5, 2)
         stiffness(5, 3)
@@ -338,7 +336,7 @@ def tile_list_mesh_contact_forces_kernel(
         response(5, 1)
         stiffness(6, 0)
         quant_h(5, 0, 256)
-        forces(256, 256, "SSSx")
+        forces(256, 256, "SSSo")
         stiffness(6, 1)
         stiffness(6, 2)
         stiffness(6, 3)
@@ -353,6 +351,6 @@ def tile_list_mesh_contact_forces_kernel(
         response(7, 0)
         response(7, 1)
         quant_h(7, 0, 128)
-        forces(768, 128, "SVVx")
+        forces(768, 128, "VSVx")
         quant_h(7, 128, 128)
         forces(896, 128, "SVSx")

@@ -56,7 +56,7 @@ def tile_list_mesh_contact_forces_kernel(
         wsc = held([P, 2 * N], U8, "wsc")
         hc = [held([P, S], U32, "hc%d" % i) for i in range(2)]
         hsc = [held([P, S], U8, "hsc%d" % i) for i in range(2)]
-        gg = held([P, 2, S], F32, "gg")
+        gg = held([P, 3, S], F32, "gg")
         one = held([P, 1], F32, "one")
         warm = held([P, 1], F32, "warm")
 
@@ -75,7 +75,7 @@ def tile_list_mesh_contact_forces_kernel(
 
         def load_table_scales():
             for q in range(4):
-                nc.gpsimd.dma_start(
+                nc.sync.dma_start(
                     out=ts[32 * q + 4 : 32 * q + 12, :].bitcast(I32), in_=tab_scales[:, 4 * q : 4 * q + 4, :].bitcast(I32)
                 )
 
@@ -192,7 +192,7 @@ def tile_list_mesh_contact_forces_kernel(
             if u not in u_of:
                 u_of[u] = ring.tile([P, PACK, width], F32, name="gr", bufs=2)
             nc.vector.tensor_tensor(
-                out=u_of[u][:, 0:2, :], in0=gg[:, :, n_lo : n_lo + width], in1=r_of[u][:, 0:2, :], op=MULT
+                out=u_of[u][:, 0:3, :], in0=gg[:, :, n_lo : n_lo + width], in1=r_of[u][:, 0:3, :], op=MULT
             )
 
         def response(u, hb):
@@ -243,78 +243,75 @@ def tile_list_mesh_contact_forces_kernel(
             if how[3] != "x":
                 nc.sync.dma_start(out=out_v[:, :, cols], in_=stage[:])
 
-        load_table_scales()
         load_words(0)
         nc.sync.dma_start(lst[:], offs)
-        load_scales(bs_raw, b4_scales)
-        load_a(0, 0)
-        nc.sync.dma_start(out=bw_raw[:].bitcast(I32), in_=b4_words[0].bitcast(I32))
+        nc.sync.dma_start(lst2[:], offs2)
+        load_table_scales()
         load_words(1)
         load_scales(ts2, tab2_scales)
-        nc.sync.dma_start(lst2[:], offs2)
+        load_a(0, 0)
         load_a(1, 0)
+        load_scales(bs_raw, b4_scales)
+        nc.sync.dma_start(out=bw_raw[:].bitcast(I32), in_=b4_words[0].bitcast(I32))
         load_words(2)
-        load_a(0, 1)
         load_g(0, 0)
         load_g(0, 1)
         load_g(0, 2)
-        load_g(0, 3)
         load_a(1, 1)
+        load_g(0, 3)
+        load_a(0, 1)
         load_w(0)
+        load_w(1)
         load_g(1, 0)
         load_g(1, 1)
-        load_w(1)
         load_g(1, 2)
         load_g(1, 3)
         cast_a(0, 0, "S")
         cast_a(1, 0, "S")
         quant_a(0, 0)
         quant_a(1, 0)
+        gather(vw[2], tw[2][:].bitcast(U32), lst2, 0, 256)
+        nc.vector.tensor_copy(out=bw[:].bitcast(U16).rearrange("p (b t m) -> p b t m", b=2, t=PACK), in_=bw_raw[:].bitcast(U16).rearrange("p (b m t) -> p b t m", b=2, t=PACK))
+        nc.vector.tensor_copy(out=bs[:].rearrange("p (b t m) -> p b t m", b=2, t=PACK), in_=bs_raw[:].rearrange("p (b m t) -> p b t m", b=2, t=PACK))
         gather(vw[0], tw[0][:].bitcast(U32), lst, 0, 1024)
         gather(vs, ts[:], lst, 0, 1024)
         gather(vw[1], tw[1][:].bitcast(U32), lst, 0, 1024)
         gather(vs2, ts2[:], lst2, 0, 1024)
-        gather(vw[2], tw[2][:].bitcast(U32), lst2, 0, 256)
-        nc.vector.tensor_copy(out=bw[:].bitcast(U16).rearrange("p (b t m) -> p b t m", b=2, t=PACK), in_=bw_raw[:].bitcast(U16).rearrange("p (b m t) -> p b t m", b=2, t=PACK))
-        nc.vector.tensor_copy(out=bs[:].rearrange("p (b t m) -> p b t m", b=2, t=PACK), in_=bs_raw[:].rearrange("p (b m t) -> p b t m", b=2, t=PACK))
-        cast_a(0, 1, "V")
         displacement(0, 1)
         gather(vw[2], tw[2][:].bitcast(U32), lst2, 256, 512)
         gather(vw[2], tw[2][:].bitcast(U32), lst2, 512, 1024)
-        quant_a(0, 1)
         gather(gg[:, 0, :], g[0][:], lst, 0, 1024)
         gather(gg[:, 1, :], g[1][:], lst, 0, 1024)
+        gather(gg[:, 2, :], g[2][:], lst, 0, 1024)
         displacement(1, 1)
+        cast_a(1, 1, "V")
+        quant_a(1, 1)
+        cast_a(0, 1, "V")
+        quant_a(0, 1)
         displacement(2, 1)
         stiffness_early(0)
-        stiffness(0, 2)
         stiffness(0, 3)
         response(0, 0)
         response(0, 1)
-        cast_a(1, 1, "V")
-        quant_a(1, 1)
-        displacement(3, 2)
+        displacement(3, 1)
         stiffness_early(1)
         quant_h(0, 0, 256)
-        stiffness(1, 2)
         stiffness(1, 3)
         response(1, 0)
         response(1, 1)
+        cast_w(0, "S")
         displacement(4, 2)
         stiffness_early(2)
         quant_h(1, 0, 256)
-        stiffness(2, 2)
         stiffness(2, 3)
         response(2, 0)
         response(2, 1)
         displacement(5, 2)
         stiffness_early(3)
         quant_h(2, 0, 256)
-        stiffness(3, 2)
         stiffness(3, 3)
         response(3, 0)
         response(3, 1)
-        cast_w(0, "S")
         cast_w(1, "S")
         displacement(6, 2)
         stiffness(4, 0)

@@ -19,8 +19,9 @@ MULT = mybir.AluOpType.mult
 P = 128
 PACK = 4
 KP = P * PACK
-UNITS = [[0,0,256],[0,256,256],[0,512,256],[0,768,256],[1,0,256],[1,256,256],[1,512,256],[1,768,256]]
 BK = 128
+RUN = 4
+EARLY = 2
 
 
 def tile_list_mesh_contact_forces_kernel(
@@ -32,8 +33,8 @@ def tile_list_mesh_contact_forces_kernel(
         ring = ctx.enter_context(tc.tile_pool(name="ring", bufs=2))
         psum = ctx.enter_context(tc.psum_pool(name="psum", bufs=1))
 
-        def held(shape, dtype, name):
-            return keep.tile(shape, dtype, name=name, align_bytes=64)
+        def held(shape, dtype, name, tag=None):
+            return keep.tile(shape, dtype, name=name, tag=tag or name, align_bytes=64)
 
         lst = keep.tile([P, S // 16], U16, name="lst")
         lst2 = keep.tile([P, S // 16], U16, name="lst2")
@@ -50,20 +51,18 @@ def tile_list_mesh_contact_forces_kernel(
         ac = [held([P, H], U32, "ac%d" % i) for i in range(2)]
         asc = [held([P, H], U8, "asc%d" % i) for i in range(2)]
         g = [held([P, T], F32, "g%d" % i) for i in range(8)]
-        w_raw = held([P, 2, PACK, N], F32, "w_raw")
-        w_bf = held([P, 2 * N * PACK], BF16, "w_bf")
-        wc = held([P, 2 * N], U32, "wc")
         wsc = held([P, 2 * N], U8, "wsc")
+        wc = {}
         hc = [held([P, S], U32, "hc%d" % i) for i in range(2)]
         hsc = [held([P, S], U8, "hsc%d" % i) for i in range(2)]
-        gg = held([P, 3, S], F32, "gg")
+        gg = held([P, EARLY, S], F32, "gg")
         one = held([P, 1], F32, "one")
         warm = held([P, 1], F32, "warm")
 
-        nc.vector.memset(one[:], 1.0)
-        nc.scalar.activation(out=warm[:], in_=one[:], func=ACT.Abs_reciprocal_sqrt, bias=one[:])
-        for plane in (ts, ts2, bs_raw):
+        for plane in (ts2, ts, bs_raw):
             nc.vector.memset(plane[:].bitcast(I32), 0)
+        nc.gpsimd.memset(one[:], 1.0)
+        nc.scalar.activation(out=warm[:], in_=one[:], func=ACT.Abs_reciprocal_sqrt, bias=one[:])
 
         def load_words(i):
             src = tab_words[i] if i < 2 else tab2_words[0]
@@ -79,34 +78,44 @@ def tile_list_mesh_contact_forces_kernel(
                     out=ts[32 * q + 4 : 32 * q + 12, :].bitcast(I32), in_=tab_scales[:, 4 * q : 4 * q + 4, :].bitcast(I32)
                 )
 
-        a_raw = {}
+        raw = {}
 
         def load_a(kp, b):
-            t = ring.tile([P, PACK, KP], F32, name="a_raw", bufs=3)
-            a_raw[kp, b] = t
+            t = ring.tile([P, PACK, KP], F32, name="a_raw", tag="raw", bufs=2)
+            raw["a", kp, b] = t
             nc.sync.dma_start(
                 out=t[:], in_=a[kp * KP : (kp + 1) * KP, b * KP : (b + 1) * KP].rearrange("(p j) c -> p j c", j=PACK)
             )
 
-        g_src = gT.rearrange("(b p t) n -> b t p n", p=P, t=PACK)
+        g_src = gT.rearrange("(b q t s) n -> b t q s n", q=P // RUN, t=PACK, s=RUN)
+        w_src = w.rearrange("(b q t s) n -> b t q s n", q=P // RUN, t=PACK, s=RUN)
 
         def load_g(b, t):
             nc.sync.dma_start(out=g[4 * b + t][:], in_=g_src[b, t])
 
         def load_w(b):
-            nc.sync.dma_start(out=w_raw[:, b], in_=w[b * KP : (b + 1) * KP, :].rearrange("(p j) n -> p j n", j=PACK))
+            t = held([P, PACK, N], F32, "w_raw%d" % b, "tw%d" % b)
+            raw["w", b] = t
+            for j in range(PACK):
+                nc.sync.dma_start(out=t[:, j, :], in_=w_src[b, j])
+
+        def negated(eng, dst, src):
+            if eng == "S":
+                nc.scalar.activation(out=dst, in_=src, func=ACT.Copy, scale=-1.0)
+            elif eng == "G":
+                nc.gpsimd.tensor_scalar(out=dst, in0=src, scalar1=-1.0, scalar2=0.0, op0=MULT, op1=mybir.AluOpType.add)
+            else:
+                nc.vector.tensor_scalar(out=dst, in0=src, scalar1=-1.0, scalar2=None, op0=MULT)
 
         a_bf = {}
 
-        def cast_a(kp, b, eng):
+        def cast_a(kp, b, engs):
             t = ring.tile([P, PACK, P, PACK], BF16, name="a_bf", bufs=2, align_bytes=64)
             a_bf[kp, b] = t
-            dst = t[:].rearrange("p t m j -> p m j t")
-            src = a_raw[kp, b][:].rearrange("p j (m t) -> p m j t", t=PACK)
-            if eng == "S":
-                nc.scalar.activation(out=dst, in_=src, func=ACT.Copy, scale=-1.0)
-            else:
-                nc.vector.tensor_scalar(out=dst, in0=src, scalar1=-1.0, scalar2=None, op0=MULT)
+            dst = t[:].rearrange("p t (q s) j -> p t q j s", s=RUN)
+            src = raw["a", kp, b][:].rearrange("p j (q t s) -> p t q j s", t=PACK, s=RUN)
+            for plane in range(PACK):
+                negated(engs[plane], dst[:, plane], src[:, plane])
 
         def quant_a(kp, b):
             cols = slice(b * KP, (b + 1) * KP)
@@ -116,18 +125,20 @@ def tile_list_mesh_contact_forces_kernel(
                 in_=a_bf[kp, b][:].rearrange("p t m j -> p (t m j)"),
             )
 
-        def cast_w(b, eng):
+        w_bf = held([P, 2 * N * PACK], BF16, "w_bf")
+
+        def cast_w(b, eng, parts):
             dst = w_bf[:, b * N * PACK : (b + 1) * N * PACK].rearrange("p (c i j) -> p c j i", i=4, j=PACK)
-            src = w_raw[:, b].rearrange("p j (c i) -> p c j i", i=4)
-            if eng == "S":
-                nc.scalar.activation(out=dst, in_=src, func=ACT.Copy, scale=-1.0)
-            else:
-                nc.vector.tensor_scalar(out=dst, in0=src, scalar1=-1.0, scalar2=None, op0=MULT)
+            src = raw["w", b][:].rearrange("p j (c i) -> p c j i", i=4)
+            step = N // 4 // parts
+            for c0 in range(0, N // 4, step):
+                negated(eng, dst[:, c0 : c0 + step], src[:, c0 : c0 + step])
 
         def quant_w():
-            for c0, c1 in ((0, 512), (512, 768)):
+            wc["codes"] = held([P, 2 * N], U32, "wc", "g0")
+            for c0, c1 in ((0, 512), (512, 2 * N)):
                 nc.vector.quantize_mx(
-                    out=wc[:, c0:c1].bitcast(FP8X4), scales=wsc[:, c0:c1], in_=w_bf[:, PACK * c0 : PACK * c1]
+                    out=wc["codes"][:, c0:c1].bitcast(FP8X4), scales=wsc[:, c0:c1], in_=w_bf[:, PACK * c0 : PACK * c1]
                 )
 
         def gather(dst, window, offsets, n0, n1):
@@ -135,17 +146,20 @@ def tile_list_mesh_contact_forces_kernel(
 
         banks = {}
         r_of = {}
+        gr_of = {}
         h_of = {}
-        u_of = {}
 
-        def displacement(u, groups):
-            b, n_lo, width = UNITS[u]
-            r = ring.tile([P, PACK, width], F32, name="r", bufs=3)
-            r_of[u] = r
-            for hb in range(width // BK):
+        def displacement(b, n_lo, width):
+            if (b, n_lo) == (0, 768):
+                r = ring.tile([P, PACK, width], F32, name="r", tag="raw", bufs=2)
+            elif (b, n_lo) == (1, 256):
+                r = held([P, PACK, width], F32, "r", "g0")
+            else:
+                r = ring.tile([P, PACK, width], F32, name="r%d" % width, bufs=(3 if width <= 256 else 1))
+            r_of[b, n_lo] = r
+            for n0 in range(n_lo, n_lo + width, BK):
                 bank = psum.tile([P, PACK, BK], F32, name="bank", bufs=8)
-                banks[u, hb] = bank
-                n0 = n_lo + hb * BK
+                banks[b, n0] = bank
                 cols = slice(n0, n0 + BK)
                 for t in range(PACK):
                     m0 = b * KP + t * P
@@ -169,65 +183,73 @@ def tile_list_mesh_contact_forces_kernel(
                         start=False,
                         stop=True,
                     )
-                nc.scalar.activation(out=r[:, :, hb * BK : (hb + 1) * BK], in_=bank[:], func=ACT.Square)
-            per = PACK // groups
-            for gi in range(groups):
-                part = r[:, gi * per : (gi + 1) * per, :]
-                nc.scalar.activation(out=part, in_=part, func=ACT.Abs_reciprocal_sqrt, bias=one[:])
-                nc.scalar.activation(out=part, in_=part, func=ACT.Square)
+                nc.scalar.activation(out=r[:, :, n0 - n_lo : n0 - n_lo + BK], in_=bank[:], func=ACT.Square)
 
-        def stiffness(u, t):
-            b, n_lo, width = UNITS[u]
-            if u not in u_of:
-                u_of[u] = ring.tile([P, PACK, width], F32, name="gr", bufs=2)
+        def influence(b, n_lo, groups):
+            squares = [r_of[b, n_lo][:, t0:t1, :] for t0, t1 in groups]
+            if (b, n_lo) == (0, 512):
+                r_of[b, n_lo] = ring.tile(list(r_of[b, n_lo].shape), F32, name="r", tag="raw", bufs=2)
+            parts = [r_of[b, n_lo][:, t0:t1, :] for t0, t1 in groups]
+            for i in range(len(parts) + 1):
+                if i < len(parts):
+                    nc.scalar.activation(out=parts[i], in_=squares[i], func=ACT.Abs_reciprocal_sqrt, bias=one[:])
+                if i > 0:
+                    nc.scalar.activation(out=parts[i - 1], in_=parts[i - 1], func=ACT.Square)
+
+        def gr_tile(b, n_lo):
+            if (b, n_lo) not in gr_of:
+                tag = "gr%d" % b
+                gr_of[b, n_lo] = ring.tile(list(r_of[b, n_lo].shape), F32, name="gr", tag=tag, bufs=2 - b, align_bytes=64)
+            return gr_of[b, n_lo]
+
+        def stiffness(b, n_lo, t, off, width):
             nc.vector.tensor_tensor(
-                out=u_of[u][:, t, :],
-                in0=g[4 * b + t][:].indirect(lst[:, n_lo // 16 : (n_lo + width) // 16]),
-                in1=r_of[u][:, t, :],
+                out=gr_tile(b, n_lo)[:, t, off : off + width],
+                in0=g[4 * b + t][:].indirect(lst[:, (n_lo + off) // 16 : (n_lo + off + width) // 16]),
+                in1=r_of[b, n_lo][:, t, off : off + width],
                 op=MULT,
             )
 
-        def stiffness_early(u):
-            b, n_lo, width = UNITS[u]
-            if u not in u_of:
-                u_of[u] = ring.tile([P, PACK, width], F32, name="gr", bufs=2)
+        def stiffness_early(n_lo, off, width):
             nc.vector.tensor_tensor(
-                out=u_of[u][:, 0:3, :], in0=gg[:, :, n_lo : n_lo + width], in1=r_of[u][:, 0:3, :], op=MULT
-            )
-
-        def response(u, hb):
-            width = UNITS[u][2]
-            if u not in h_of:
-                h_of[u] = ring.tile([P, width, PACK], BF16, name="h_bf", bufs=2, align_bytes=64)
-            cols = slice(hb * BK, (hb + 1) * BK)
-            nc.vector.tensor_tensor(
-                out=h_of[u][:, cols, :].rearrange("p (c i) t -> p c t i", i=4),
-                in0=banks[u, hb][:].rearrange("p t (c i) -> p c t i", i=4),
-                in1=u_of[u][:, :, cols].rearrange("p t (c i) -> p c t i", i=4),
+                out=gr_tile(0, n_lo)[:, 0:EARLY, off : off + width],
+                in0=gg[:, :, n_lo + off : n_lo + off + width],
+                in1=r_of[0, n_lo][:, 0:EARLY, off : off + width],
                 op=MULT,
             )
 
-        def quant_h(u, off, width):
-            b, n_lo = UNITS[u][:2]
+        def response(b, n_lo, off):
+            gr = gr_of[b, n_lo]
+            if (b, n_lo) not in h_of:
+                h_of[b, n_lo] = ring.tile([P, gr.shape[2], PACK], BF16, name="h_bf", bufs=2, align_bytes=64)
+            cols = slice(off, off + BK)
+            nc.vector.tensor_tensor(
+                out=h_of[b, n_lo][:, cols, :].rearrange("p (c i) t -> p c t i", i=4),
+                in0=banks[b, n_lo + off][:].rearrange("p t (c i) -> p c t i", i=4),
+                in1=gr[:, :, cols].rearrange("p t (c i) -> p c t i", i=4),
+                op=MULT,
+            )
+
+        def quant_h(b, n_lo, off, width):
             cols = slice(n_lo + off, n_lo + off + width)
             nc.vector.quantize_mx(
                 out=hc[b][:, cols].bitcast(FP8X4),
                 scales=hsc[b][:, cols],
-                in_=h_of[u][:, off : off + width, :].rearrange("p n t -> p (n t)"),
+                in_=h_of[b, n_lo][:, off : off + width, :].rearrange("p n t -> p (n t)"),
             )
 
         out_v = out.rearrange("(c p) j -> p c j", p=P)
 
         def forces(n_lo, width, how):
             cols = slice(n_lo, n_lo + width)
-            stage = ring.tile([P, N // P, width], F32, name="stage", bufs=3)
+            stage = ring.tile([P, N // P, width], F32, name="stage", tag="raw" if width > BK else "stage", bufs=2)
             for c in range(N // P):
                 acc = psum.tile([P, width], F32, name="bank", bufs=8)
                 for b in range(2):
                     rows = slice(b * N + c * P, b * N + (c + 1) * P)
                     nc.tensor.matmul_mx(
                         out=acc[:],
-                        lhsT=wc[:, rows].bitcast(FP8X4),
+                        lhsT=wc["codes"][:, rows].bitcast(FP8X4),
                         lhsT_scale=wsc[:, rows],
                         rhs=hc[b][:, cols].bitcast(FP8X4),
                         rhs_scale=hsc[b][:, cols],
@@ -243,111 +265,97 @@ def tile_list_mesh_contact_forces_kernel(
             if how[3] != "x":
                 nc.sync.dma_start(out=out_v[:, :, cols], in_=stage[:])
 
-        load_words(0)
-        nc.sync.dma_start(lst[:], offs)
+        def deal_b4():
+            nc.vector.tensor_copy(
+                out=bw[:].bitcast(I32).rearrange("p (b t q e) -> p b t q e", b=2, t=PACK, e=2),
+                in_=bw_raw[:].bitcast(I32).rearrange("p (b q t e) -> p b t q e", b=2, t=PACK, e=2),
+            )
+            nc.vector.tensor_copy(
+                out=bs[:].bitcast(I32).rearrange("p (b t q) -> p b t q", b=2, t=PACK),
+                in_=bs_raw[:].bitcast(I32).rearrange("p (b q t) -> p b t q", b=2, t=PACK),
+            )
+
         nc.sync.dma_start(lst2[:], offs2)
-        load_table_scales()
-        load_words(1)
+        nc.sync.dma_start(lst[:], offs)
         load_scales(ts2, tab2_scales)
+        load_words(0)
+        load_table_scales()
         load_a(0, 0)
+        load_words(1)
         load_a(1, 0)
         load_scales(bs_raw, b4_scales)
         nc.sync.dma_start(out=bw_raw[:].bitcast(I32), in_=b4_words[0].bitcast(I32))
         load_words(2)
-        load_g(0, 0)
-        load_g(0, 1)
-        load_g(0, 2)
-        load_a(1, 1)
-        load_g(0, 3)
+        for t in range(PACK):
+            load_g(0, t)
+        cast_a(0, 0, "SSSS")
+        cast_a(1, 0, "SSVV")
         load_a(0, 1)
+        load_a(1, 1)
         load_w(0)
         load_w(1)
-        load_g(1, 0)
-        load_g(1, 1)
-        load_g(1, 2)
-        load_g(1, 3)
-        cast_a(0, 0, "S")
-        cast_a(1, 0, "S")
+        for t in range(PACK):
+            load_g(1, t)
         quant_a(0, 0)
         quant_a(1, 0)
         gather(vw[2], tw[2][:].bitcast(U32), lst2, 0, 256)
-        nc.vector.tensor_copy(out=bw[:].bitcast(U16).rearrange("p (b t m) -> p b t m", b=2, t=PACK), in_=bw_raw[:].bitcast(U16).rearrange("p (b m t) -> p b t m", b=2, t=PACK))
-        nc.vector.tensor_copy(out=bs[:].rearrange("p (b t m) -> p b t m", b=2, t=PACK), in_=bs_raw[:].rearrange("p (b m t) -> p b t m", b=2, t=PACK))
-        gather(vw[0], tw[0][:].bitcast(U32), lst, 0, 1024)
-        gather(vs, ts[:], lst, 0, 1024)
-        gather(vw[1], tw[1][:].bitcast(U32), lst, 0, 1024)
-        gather(vs2, ts2[:], lst2, 0, 1024)
-        displacement(0, 1)
-        gather(vw[2], tw[2][:].bitcast(U32), lst2, 256, 512)
-        gather(vw[2], tw[2][:].bitcast(U32), lst2, 512, 1024)
-        gather(gg[:, 0, :], g[0][:], lst, 0, 1024)
-        gather(gg[:, 1, :], g[1][:], lst, 0, 1024)
-        gather(gg[:, 2, :], g[2][:], lst, 0, 1024)
-        displacement(1, 1)
-        cast_a(1, 1, "V")
-        quant_a(1, 1)
-        cast_a(0, 1, "V")
+        deal_b4()
+        gather(vs2, ts2[:], lst2, 0, S)
+        gather(vw[0], tw[0][:].bitcast(U32), lst, 0, S)
+        gather(vs, ts[:], lst, 0, S)
+        gather(vw[1], tw[1][:].bitcast(U32), lst, 0, S)
+        displacement(0, 0, 256)
+        influence(0, 0, ((EARLY, PACK), (0, EARLY)))
+        gather(vw[2], tw[2][:].bitcast(U32), lst2, 256, S)
+        for t in range(EARLY):
+            gather(gg[:, t, :], g[t][:], lst, 0, S)
+        displacement(0, 256, 256)
+        influence(0, 256, ((EARLY, PACK), (0, EARLY)))
+        displacement(0, 512, 256)
+        cast_a(0, 1, "SSSS")
+        influence(0, 512, ((EARLY, PACK), (0, EARLY)))
         quant_a(0, 1)
-        displacement(2, 1)
-        stiffness_early(0)
-        stiffness(0, 3)
-        response(0, 0)
-        response(0, 1)
-        displacement(3, 1)
-        stiffness_early(1)
-        quant_h(0, 0, 256)
-        stiffness(1, 3)
-        response(1, 0)
-        response(1, 1)
-        cast_w(0, "S")
-        displacement(4, 2)
-        stiffness_early(2)
-        quant_h(1, 0, 256)
-        stiffness(2, 3)
-        response(2, 0)
-        response(2, 1)
-        displacement(5, 2)
-        stiffness_early(3)
-        quant_h(2, 0, 256)
-        stiffness(3, 3)
-        response(3, 0)
-        response(3, 1)
-        cast_w(1, "S")
-        displacement(6, 2)
-        stiffness(4, 0)
-        quant_h(3, 0, 256)
-        stiffness(4, 1)
-        stiffness(4, 2)
-        stiffness(4, 3)
-        response(4, 0)
-        response(4, 1)
+        cast_a(1, 1, "VVVV")
+        quant_a(1, 1)
+        displacement(0, 768, 256)
+        influence(0, 768, ((EARLY, PACK), (0, EARLY)))
+        for n_lo in range(0, S, 256):
+            for t in range(EARLY, PACK):
+                stiffness(0, n_lo, t, 0, 256)
+            for off in (0, BK):
+                stiffness_early(n_lo, off, BK)
+            for off in (0, BK):
+                response(0, n_lo, off)
+            for off in (0, BK):
+                quant_h(0, n_lo, off, BK)
+        for n_lo in (0, 256):
+            displacement(1, n_lo, 256)
+            influence(1, n_lo, ((0, 2), (2, PACK)))
+        cast_w(0, "S", 4)
+        cast_w(1, "V", 1)
+        displacement(1, 512, 512)
+        influence(1, 512, [(t, t + 1) for t in range(PACK)])
+        for n_lo in (0, 256):
+            for t in range(3):
+                stiffness(1, n_lo, t, 0, 256)
+            for off in (0, BK):
+                stiffness(1, n_lo, 3, off, BK)
+            for off in (0, BK):
+                response(1, n_lo, off)
+            for off in (0, BK):
+                quant_h(1, n_lo, off, BK)
         quant_w()
-        displacement(7, 2)
-        stiffness(5, 0)
-        quant_h(4, 0, 256)
-        forces(0, 256, "SSSo")
-        stiffness(5, 1)
-        stiffness(5, 2)
-        stiffness(5, 3)
-        response(5, 0)
-        response(5, 1)
-        stiffness(6, 0)
-        quant_h(5, 0, 256)
-        forces(256, 256, "SSSo")
-        stiffness(6, 1)
-        stiffness(6, 2)
-        stiffness(6, 3)
-        response(6, 0)
-        response(6, 1)
-        stiffness(7, 0)
-        quant_h(6, 0, 256)
+        forces(0, 512, "SSSo")
+        for t in (0, 1, 2):
+            stiffness(1, 512, t, 0, 512)
+        stiffness(1, 512, 3, 0, 256)
+        stiffness(1, 512, 3, 256, 256)
+        for off in (0, BK, 2 * BK):
+            response(1, 512, off)
+        quant_h(1, 512, 0, 256)
+        response(1, 512, 3 * BK)
+        quant_h(1, 512, 256, BK)
+        quant_h(1, 512, 384, BK)
         forces(512, 256, "SSSo")
-        stiffness(7, 1)
-        stiffness(7, 2)
-        stiffness(7, 3)
-        response(7, 0)
-        response(7, 1)
-        quant_h(7, 0, 128)
-        forces(768, 128, "VSVx")
-        quant_h(7, 128, 128)
-        forces(896, 128, "SVSx")
+        forces(768, 128, "SVVx")
+        forces(896, 128, "VSVx")

@@ -18,10 +18,14 @@ MULT = mybir.AluOpType.mult
 
 P = 128
 PACK = 4
-KP = P * PACK
-BK = 128
+PASS = P * PACK
 RUN = 4
+BANK = 128
+STEP = 2 * BANK
+STEPS = range(0, S, STEP)
+LIST_ROWS = 16
 EARLY = 2
+W_PIECES = 4
 
 
 def tile_list_mesh_contact_forces_kernel(
@@ -36,326 +40,304 @@ def tile_list_mesh_contact_forces_kernel(
         def held(shape, dtype, name, tag=None):
             return keep.tile(shape, dtype, name=name, tag=tag or name, align_bytes=64)
 
-        lst = keep.tile([P, S // 16], U16, name="lst")
-        lst2 = keep.tile([P, S // 16], U16, name="lst2")
-        tw = [held([P, T], I32, "tw%d" % i) for i in range(3)]
-        ts = held([P, T], U8, "ts")
-        ts2 = held([P, T], U8, "ts2")
-        bw_raw = held([P, 2 * H], U8, "bw_raw")
-        bs_raw = held([P, H], U8, "bs_raw")
-        bw = held([P, 2 * H], U8, "bw")
-        bs = held([P, H], U8, "bs")
-        vw = [held([P, S], U32, "vw%d" % i) for i in range(3)]
-        vs = held([P, S], U8, "vs")
-        vs2 = held([P, S], U8, "vs2")
-        ac = [held([P, H], U32, "ac%d" % i) for i in range(2)]
-        asc = [held([P, H], U8, "asc%d" % i) for i in range(2)]
-        g = [held([P, T], F32, "g%d" % i) for i in range(8)]
-        wsc = held([P, 2 * N], U8, "wsc")
-        wc = {}
-        hc = [held([P, S], U32, "hc%d" % i) for i in range(2)]
-        hsc = [held([P, S], U8, "hsc%d" % i) for i in range(2)]
-        gg = held([P, EARLY, S], F32, "gg")
+        def spare(shape, name):
+            return ring.tile(shape, F32, name=name, tag="spare", bufs=2)
+
+        idx = keep.tile([P, S // LIST_ROWS], U16, name="idx")
+        idx2 = keep.tile([P, S // LIST_ROWS], U16, name="idx2")
+        table_words = [held([P, T], I32, "table_words%d" % i) for i in range(3)]
+        v_table_scales = held([P, T], U8, "v_table_scales")
+        v2_table_scales = held([P, T], U8, "v2_table_scales")
+        b4_words_in = held([P, 2 * H], U8, "b4_words_in")
+        b4_scales_in = held([P, H], U8, "b4_scales_in")
+        b4_codes = held([P, 2 * H], U8, "b4_codes")
+        b4_scale = held([P, H], U8, "b4_scale")
+        picked_words = [held([P, S], U32, "picked_words%d" % i) for i in range(3)]
+        v_scale = held([P, S], U8, "v_scale")
+        v2_scale = held([P, S], U8, "v2_scale")
+        a_codes = [held([P, H], U32, "a_codes%d" % i) for i in range(2)]
+        a_scale = [held([P, H], U8, "a_scale%d" % i) for i in range(2)]
+        g_table = [held([P, T], F32, "g_table%d" % i) for i in range(2 * PACK)]
+        w_scale = held([P, 2 * N], U8, "w_scale")
+        h_codes = [held([P, S], U32, "h_codes%d" % i) for i in range(2)]
+        h_scale = [held([P, S], U8, "h_scale%d" % i) for i in range(2)]
+        g_early = held([P, EARLY, S], F32, "g_early")
         one = held([P, 1], F32, "one")
         warm = held([P, 1], F32, "warm")
 
-        for plane in (ts2, ts, bs_raw):
-            nc.vector.memset(plane[:].bitcast(I32), 0)
+        for scales in (v2_table_scales, v_table_scales, b4_scales_in):
+            nc.vector.memset(scales[:].bitcast(I32), 0)
         nc.gpsimd.memset(one[:], 1.0)
         nc.scalar.activation(out=warm[:], in_=one[:], func=ACT.Abs_reciprocal_sqrt, bias=one[:])
 
         def load_words(i):
             src = tab_words[i] if i < 2 else tab2_words[0]
-            nc.sync.dma_start(out=tw[i][:], in_=src.rearrange("p t i -> p (t i)").bitcast(I32))
+            nc.sync.dma_start(out=table_words[i][:], in_=src.rearrange("p t i -> p (t i)").bitcast(I32))
 
-        def load_scales(plane, src):
+        def load_scales(scales, src):
             for r in range(4):
-                nc.sync.dma_start(out=plane[r:P:32, :].bitcast(I32), in_=src[0, r:16:4, :].bitcast(I32))
+                nc.sync.dma_start(out=scales[r:P:32, :].bitcast(I32), in_=src[0, r:16:4, :].bitcast(I32))
 
-        def load_table_scales():
-            for q in range(4):
+        def load_v_scales():
+            for quad in range(4):
                 nc.sync.dma_start(
-                    out=ts[32 * q + 4 : 32 * q + 12, :].bitcast(I32), in_=tab_scales[:, 4 * q : 4 * q + 4, :].bitcast(I32)
+                    out=v_table_scales[32 * quad + 4 : 32 * quad + 12, :].bitcast(I32),
+                    in_=tab_scales[:, 4 * quad : 4 * quad + 4, :].bitcast(I32),
                 )
 
-        raw = {}
+        def load_a(n, half):
+            quarter = spare([P, PACK, PASS], "a_in")
+            src = a[n * PASS : (n + 1) * PASS, half * PASS : (half + 1) * PASS]
+            nc.sync.dma_start(out=quarter[:], in_=src.rearrange("(p j) c -> p j c", j=PACK))
+            return quarter
 
-        def load_a(kp, b):
-            t = ring.tile([P, PACK, KP], F32, name="a_raw", tag="raw", bufs=2)
-            raw["a", kp, b] = t
-            nc.sync.dma_start(
-                out=t[:], in_=a[kp * KP : (kp + 1) * KP, b * KP : (b + 1) * KP].rearrange("(p j) c -> p j c", j=PACK)
-            )
+        g_planes = gT.rearrange("(h q t s) n -> h t q s n", q=P // RUN, t=PACK, s=RUN)
+        w_planes = w.rearrange("(h q t s) n -> h t q s n", q=P // RUN, t=PACK, s=RUN)
 
-        g_src = gT.rearrange("(b q t s) n -> b t q s n", q=P // RUN, t=PACK, s=RUN)
-        w_src = w.rearrange("(b q t s) n -> b t q s n", q=P // RUN, t=PACK, s=RUN)
+        def load_g(half):
+            for t in range(PACK):
+                nc.sync.dma_start(out=g_table[PACK * half + t][:], in_=g_planes[half, t])
 
-        def load_g(b, t):
-            nc.sync.dma_start(out=g[4 * b + t][:], in_=g_src[b, t])
+        def load_w(half):
+            w_in = held([P, PACK, N], F32, "w_in%d" % half, "table_words%d" % half)
+            for t in range(PACK):
+                nc.sync.dma_start(out=w_in[:, t, :], in_=w_planes[half, t])
+            return w_in
 
-        def load_w(b):
-            t = held([P, PACK, N], F32, "w_raw%d" % b, "tw%d" % b)
-            raw["w", b] = t
-            for j in range(PACK):
-                nc.sync.dma_start(out=t[:, j, :], in_=w_src[b, j])
-
-        def negated(eng, dst, src):
-            if eng == "S":
-                nc.scalar.activation(out=dst, in_=src, func=ACT.Copy, scale=-1.0)
-            elif eng == "G":
-                nc.gpsimd.tensor_scalar(out=dst, in0=src, scalar1=-1.0, scalar2=0.0, op0=MULT, op1=mybir.AluOpType.add)
-            else:
+        def negate(on_vector, dst, src):
+            if on_vector:
                 nc.vector.tensor_scalar(out=dst, in0=src, scalar1=-1.0, scalar2=None, op0=MULT)
+            else:
+                nc.scalar.activation(out=dst, in_=src, func=ACT.Copy, scale=-1.0)
 
-        a_bf = {}
+        def round_a(quarter, planes_on_scalar):
+            rounded = ring.tile([P, PACK, P, PACK], BF16, name="a_rounded", bufs=2, align_bytes=64)
+            dst = rounded[:].rearrange("p t (q s) j -> p t q j s", s=RUN)
+            src = quarter[:].rearrange("p j (q t s) -> p t q j s", t=PACK, s=RUN)
+            for t in range(PACK):
+                negate(t >= planes_on_scalar, dst[:, t], src[:, t])
+            return rounded
 
-        def cast_a(kp, b, engs):
-            t = ring.tile([P, PACK, P, PACK], BF16, name="a_bf", bufs=2, align_bytes=64)
-            a_bf[kp, b] = t
-            dst = t[:].rearrange("p t (q s) j -> p t q j s", s=RUN)
-            src = raw["a", kp, b][:].rearrange("p j (q t s) -> p t q j s", t=PACK, s=RUN)
-            for plane in range(PACK):
-                negated(engs[plane], dst[:, plane], src[:, plane])
-
-        def quant_a(kp, b):
-            cols = slice(b * KP, (b + 1) * KP)
+        def quantise_a(n, half, rounded):
+            cols = slice(half * PASS, (half + 1) * PASS)
             nc.vector.quantize_mx(
-                out=ac[kp][:, cols].bitcast(FP8X4),
-                scales=asc[kp][:, cols],
-                in_=a_bf[kp, b][:].rearrange("p t m j -> p (t m j)"),
+                out=a_codes[n][:, cols].bitcast(FP8X4),
+                scales=a_scale[n][:, cols],
+                in_=rounded[:].rearrange("p t m j -> p (t m j)"),
             )
 
-        w_bf = held([P, 2 * N * PACK], BF16, "w_bf")
+        w_rounded = held([P, 2 * N * PACK], BF16, "w_rounded")
 
-        def cast_w(b, eng, parts):
-            dst = w_bf[:, b * N * PACK : (b + 1) * N * PACK].rearrange("p (c i j) -> p c j i", i=4, j=PACK)
-            src = raw["w", b][:].rearrange("p j (c i) -> p c j i", i=4)
-            step = N // 4 // parts
-            for c0 in range(0, N // 4, step):
-                negated(eng, dst[:, c0 : c0 + step], src[:, c0 : c0 + step])
+        def round_w(half, w_in):
+            dst = w_rounded[:, half * N * PACK : (half + 1) * N * PACK].rearrange("p (c i t) -> p c t i", i=RUN, t=PACK)
+            src = w_in[:].rearrange("p t (c i) -> p c t i", i=RUN)
+            width = N // RUN // W_PIECES
+            for piece in range(W_PIECES):
+                part = slice(piece * width, (piece + 1) * width)
+                negate((half, piece) == (1, W_PIECES - 1), dst[:, part], src[:, part])
 
-        def quant_w():
-            wc["codes"] = held([P, 2 * N], U32, "wc", "g0")
-            for c0, c1 in ((0, 512), (512, 2 * N)):
+        def quantise_w(tag):
+            w_codes = held([P, 2 * N], U32, "w_codes", tag)
+            for c0, c1 in ((0, PASS), (PASS, 2 * N)):
                 nc.vector.quantize_mx(
-                    out=wc["codes"][:, c0:c1].bitcast(FP8X4), scales=wsc[:, c0:c1], in_=w_bf[:, PACK * c0 : PACK * c1]
+                    out=w_codes[:, c0:c1].bitcast(FP8X4),
+                    scales=w_scale[:, c0:c1],
+                    in_=w_rounded[:, PACK * c0 : PACK * c1],
                 )
+            return w_codes
 
-        def gather(dst, window, offsets, n0, n1):
-            nc.vector.tensor_copy(out=dst[:, n0:n1], in_=window.indirect(offsets[:, n0 // 16 : n1 // 16]))
+        def deal_b4():
+            nc.vector.tensor_copy(
+                out=b4_codes[:].bitcast(I32).rearrange("p (h t q e) -> p h t q e", h=2, t=PACK, e=2),
+                in_=b4_words_in[:].bitcast(I32).rearrange("p (h q t e) -> p h t q e", h=2, t=PACK, e=2),
+            )
+            nc.vector.tensor_copy(
+                out=b4_scale[:].bitcast(I32).rearrange("p (h t q) -> p h t q", h=2, t=PACK),
+                in_=b4_scales_in[:].bitcast(I32).rearrange("p (h q t) -> p h t q", h=2, t=PACK),
+            )
+
+        def entries(lst, first, count):
+            return lst[:, first // LIST_ROWS : (first + count) // LIST_ROWS]
+
+        def gather(dst, table, lst, first, count):
+            nc.vector.tensor_copy(out=dst[:, first : first + count], in_=table.indirect(entries(lst, first, count)))
 
         banks = {}
-        r_of = {}
-        gr_of = {}
-        h_of = {}
+        influence = {}
 
-        def displacement(b, n_lo, width):
-            if (b, n_lo) == (0, 768):
-                r = ring.tile([P, PACK, width], F32, name="r", tag="raw", bufs=2)
-            elif (b, n_lo) == (1, 256):
-                r = held([P, PACK, width], F32, "r", "g0")
-            else:
-                r = ring.tile([P, PACK, width], F32, name="r%d" % width, bufs=(3 if width <= 256 else 1))
-            r_of[b, n_lo] = r
-            for n0 in range(n_lo, n_lo + width, BK):
-                bank = psum.tile([P, PACK, BK], F32, name="bank", bufs=8)
-                banks[b, n0] = bank
-                cols = slice(n0, n0 + BK)
+        def step_tile():
+            return ring.tile([P, PACK, STEP], F32, name="squares", bufs=3)
+
+        def displacement(half, first, squares):
+            for n0 in range(first, first + STEP, BANK):
+                bank = psum.tile([P, PACK, BANK], F32, name="bank", bufs=8)
+                banks[half, n0] = bank
+                cols = slice(n0, n0 + BANK)
                 for t in range(PACK):
-                    m0 = b * KP + t * P
+                    m0 = half * PASS + t * P
                     rows = slice(m0, m0 + P)
-                    for kp in range(2):
+                    for n in range(2):
                         nc.tensor.matmul_mx(
                             out=bank[:, t, :],
-                            lhsT=ac[kp][:, rows].bitcast(FP8X4),
-                            lhsT_scale=asc[kp][:, rows],
-                            rhs=vw[kp][:, cols].bitcast(FP8X4),
-                            rhs_scale=vs[4 + 4 * kp :, cols],
-                            start=(kp == 0),
+                            lhsT=a_codes[n][:, rows].bitcast(FP8X4),
+                            lhsT_scale=a_scale[n][:, rows],
+                            rhs=picked_words[n][:, cols].bitcast(FP8X4),
+                            rhs_scale=v_scale[4 + 4 * n :, cols],
+                            start=(n == 0),
                             stop=False,
                         )
                     nc.tensor.matmul_mx(
                         out=bank[:, t, :],
-                        lhsT=bw[:, 2 * m0 : 2 * (m0 + P)].bitcast(FP4X4),
-                        lhsT_scale=bs[:, rows],
-                        rhs=vw[2][:, cols].bitcast(FP8X4),
-                        rhs_scale=vs2[:, cols],
+                        lhsT=b4_codes[:, 2 * m0 : 2 * (m0 + P)].bitcast(FP4X4),
+                        lhsT_scale=b4_scale[:, rows],
+                        rhs=picked_words[2][:, cols].bitcast(FP8X4),
+                        rhs_scale=v2_scale[:, cols],
                         start=False,
                         stop=True,
                     )
-                nc.scalar.activation(out=r[:, :, n0 - n_lo : n0 - n_lo + BK], in_=bank[:], func=ACT.Square)
+                nc.scalar.activation(out=squares[:, :, n0 - first : n0 - first + BANK], in_=bank[:], func=ACT.Square)
+            return squares
 
-        def influence(b, n_lo, groups):
-            squares = [r_of[b, n_lo][:, t0:t1, :] for t0, t1 in groups]
-            if (b, n_lo) == (0, 512):
-                r_of[b, n_lo] = ring.tile(list(r_of[b, n_lo].shape), F32, name="r", tag="raw", bufs=2)
-            parts = [r_of[b, n_lo][:, t0:t1, :] for t0, t1 in groups]
-            for i in range(len(parts) + 1):
-                if i < len(parts):
-                    nc.scalar.activation(out=parts[i], in_=squares[i], func=ACT.Abs_reciprocal_sqrt, bias=one[:])
-                if i > 0:
-                    nc.scalar.activation(out=parts[i - 1], in_=parts[i - 1], func=ACT.Square)
+        def invert(half, first, squares, result):
+            influence[half, first] = result
+            groups = (slice(EARLY, PACK), slice(0, EARLY)) if half == 0 else (slice(0, 2), slice(2, PACK))
+            for planes in groups:
+                nc.scalar.activation(
+                    out=result[:, planes, :], in_=squares[:, planes, :], func=ACT.Abs_reciprocal_sqrt, bias=one[:]
+                )
+            for planes in groups:
+                nc.scalar.activation(out=result[:, planes, :], in_=result[:, planes, :], func=ACT.Square)
 
-        def gr_tile(b, n_lo):
-            if (b, n_lo) not in gr_of:
-                tag = "gr%d" % b
-                gr_of[b, n_lo] = ring.tile(list(r_of[b, n_lo].shape), F32, name="gr", tag=tag, bufs=2 - b, align_bytes=64)
-            return gr_of[b, n_lo]
+        def scalar_step(half, first, tile):
+            invert(half, first, displacement(half, first, tile), tile)
 
-        def stiffness(b, n_lo, t, off, width):
-            nc.vector.tensor_tensor(
-                out=gr_tile(b, n_lo)[:, t, off : off + width],
-                in0=g[4 * b + t][:].indirect(lst[:, (n_lo + off) // 16 : (n_lo + off + width) // 16]),
-                in1=r_of[b, n_lo][:, t, off : off + width],
-                op=MULT,
-            )
+        def vector_step(half, first):
+            weight = ring.tile([P, PACK, STEP], F32, name="weight", bufs=1, align_bytes=64)
+            infl = influence[half, first]
 
-        def stiffness_early(n_lo, off, width):
-            nc.vector.tensor_tensor(
-                out=gr_tile(0, n_lo)[:, 0:EARLY, off : off + width],
-                in0=gg[:, :, n_lo + off : n_lo + off + width],
-                in1=r_of[0, n_lo][:, 0:EARLY, off : off + width],
-                op=MULT,
-            )
+            def gather_times_influence(t, off, count):
+                nc.vector.tensor_tensor(
+                    out=weight[:, t, off : off + count],
+                    in0=g_table[PACK * half + t][:].indirect(entries(idx, first + off, count)),
+                    in1=infl[:, t, off : off + count],
+                    op=MULT,
+                )
 
-        def response(b, n_lo, off):
-            gr = gr_of[b, n_lo]
-            if (b, n_lo) not in h_of:
-                h_of[b, n_lo] = ring.tile([P, gr.shape[2], PACK], BF16, name="h_bf", bufs=2, align_bytes=64)
-            cols = slice(off, off + BK)
-            nc.vector.tensor_tensor(
-                out=h_of[b, n_lo][:, cols, :].rearrange("p (c i) t -> p c t i", i=4),
-                in0=banks[b, n_lo + off][:].rearrange("p t (c i) -> p c t i", i=4),
-                in1=gr[:, :, cols].rearrange("p t (c i) -> p c t i", i=4),
-                op=MULT,
-            )
+            if half == 0:
+                for t in range(EARLY, PACK):
+                    gather_times_influence(t, 0, STEP)
+                for off in (0, BANK):
+                    nc.vector.tensor_tensor(
+                        out=weight[:, 0:EARLY, off : off + BANK],
+                        in0=g_early[:, :, first + off : first + off + BANK],
+                        in1=infl[:, 0:EARLY, off : off + BANK],
+                        op=MULT,
+                    )
+            else:
+                for t in range(PACK - 1):
+                    gather_times_influence(t, 0, STEP)
+                for off in (0, BANK):
+                    gather_times_influence(PACK - 1, off, BANK)
+            h_rounded = ring.tile([P, STEP, PACK], BF16, name="h_rounded", bufs=2, align_bytes=64)
+            for off in (0, BANK):
+                cols = slice(off, off + BANK)
+                nc.vector.tensor_tensor(
+                    out=h_rounded[:, cols, :].rearrange("p (c i) t -> p c t i", i=RUN),
+                    in0=banks[half, first + off][:].rearrange("p t (c i) -> p c t i", i=RUN),
+                    in1=weight[:, :, cols].rearrange("p t (c i) -> p c t i", i=RUN),
+                    op=MULT,
+                )
+            for off in (0, BANK):
+                cols = slice(first + off, first + off + BANK)
+                nc.vector.quantize_mx(
+                    out=h_codes[half][:, cols].bitcast(FP8X4),
+                    scales=h_scale[half][:, cols],
+                    in_=h_rounded[:, off : off + BANK, :].rearrange("p n t -> p (n t)"),
+                )
 
-        def quant_h(b, n_lo, off, width):
-            cols = slice(n_lo + off, n_lo + off + width)
-            nc.vector.quantize_mx(
-                out=hc[b][:, cols].bitcast(FP8X4),
-                scales=hsc[b][:, cols],
-                in_=h_of[b, n_lo][:, off : off + width, :].rearrange("p n t -> p (n t)"),
-            )
+        out_rows = out.rearrange("(c p) j -> p c j", p=P)
 
-        out_v = out.rearrange("(c p) j -> p c j", p=P)
-
-        def forces(n_lo, width, how):
-            cols = slice(n_lo, n_lo + width)
-            stage = ring.tile([P, N // P, width], F32, name="stage", tag="raw" if width > BK else "stage", bufs=2)
+        def forces(w_codes, first, count, blocks_on_vector):
+            cols = slice(first, first + count)
+            if count > BANK:
+                stage = spare([P, N // P, count], "wide_stage")
+            else:
+                stage = ring.tile([P, N // P, count], F32, name="stage", bufs=2)
             for c in range(N // P):
-                acc = psum.tile([P, width], F32, name="bank", bufs=8)
-                for b in range(2):
-                    rows = slice(b * N + c * P, b * N + (c + 1) * P)
+                acc = psum.tile([P, count], F32, name="bank", bufs=8)
+                for half in range(2):
+                    rows = slice(half * N + c * P, half * N + (c + 1) * P)
                     nc.tensor.matmul_mx(
                         out=acc[:],
-                        lhsT=wc["codes"][:, rows].bitcast(FP8X4),
-                        lhsT_scale=wsc[:, rows],
-                        rhs=hc[b][:, cols].bitcast(FP8X4),
-                        rhs_scale=hsc[b][:, cols],
-                        start=(b == 0),
-                        stop=(b == 1),
+                        lhsT=w_codes[:, rows].bitcast(FP8X4),
+                        lhsT_scale=w_scale[:, rows],
+                        rhs=h_codes[half][:, cols].bitcast(FP8X4),
+                        rhs_scale=h_scale[half][:, cols],
+                        start=(half == 0),
+                        stop=(half == 1),
                     )
-                if how[c] == "S":
-                    nc.scalar.copy(out=stage[:, c, :], in_=acc[:])
-                else:
+                if c in blocks_on_vector:
                     nc.vector.tensor_copy(out=stage[:, c, :], in_=acc[:])
-                if how[3] == "x":
-                    nc.sync.dma_start(out=out_v[:, c, cols], in_=stage[:, c, :])
-            if how[3] != "x":
-                nc.sync.dma_start(out=out_v[:, :, cols], in_=stage[:])
+                else:
+                    nc.scalar.copy(out=stage[:, c, :], in_=acc[:])
+            nc.sync.dma_start(out=out_rows[:, :, cols], in_=stage[:])
 
-        def deal_b4():
-            nc.vector.tensor_copy(
-                out=bw[:].bitcast(I32).rearrange("p (b t q e) -> p b t q e", b=2, t=PACK, e=2),
-                in_=bw_raw[:].bitcast(I32).rearrange("p (b q t e) -> p b t q e", b=2, t=PACK, e=2),
-            )
-            nc.vector.tensor_copy(
-                out=bs[:].bitcast(I32).rearrange("p (b t q) -> p b t q", b=2, t=PACK),
-                in_=bs_raw[:].bitcast(I32).rearrange("p (b q t) -> p b t q", b=2, t=PACK),
-            )
-
-        nc.sync.dma_start(lst2[:], offs2)
-        nc.sync.dma_start(lst[:], offs)
-        load_scales(ts2, tab2_scales)
+        nc.sync.dma_start(idx2[:], offs2)
+        nc.sync.dma_start(idx[:], offs)
+        load_scales(v2_table_scales, tab2_scales)
         load_words(0)
-        load_table_scales()
-        load_a(0, 0)
+        load_v_scales()
+        a_00 = load_a(0, 0)
         load_words(1)
-        load_a(1, 0)
-        load_scales(bs_raw, b4_scales)
-        nc.sync.dma_start(out=bw_raw[:].bitcast(I32), in_=b4_words[0].bitcast(I32))
+        a_10 = load_a(1, 0)
+        load_scales(b4_scales_in, b4_scales)
+        nc.sync.dma_start(out=b4_words_in[:].bitcast(I32), in_=b4_words[0].bitcast(I32))
         load_words(2)
-        for t in range(PACK):
-            load_g(0, t)
-        cast_a(0, 0, "SSSS")
-        cast_a(1, 0, "SSVV")
-        load_a(0, 1)
-        load_a(1, 1)
-        load_w(0)
-        load_w(1)
-        for t in range(PACK):
-            load_g(1, t)
-        quant_a(0, 0)
-        quant_a(1, 0)
-        gather(vw[2], tw[2][:].bitcast(U32), lst2, 0, 256)
+        load_g(0)
+        rounded_00 = round_a(a_00, PACK)
+        rounded_10 = round_a(a_10, PACK // 2)
+        a_01 = load_a(0, 1)
+        a_11 = load_a(1, 1)
+        w_in = [load_w(0), load_w(1)]
+        load_g(1)
+
+        quantise_a(0, 0, rounded_00)
+        quantise_a(1, 0, rounded_10)
+        gather(picked_words[2], table_words[2][:].bitcast(U32), idx2, 0, STEP)
         deal_b4()
-        gather(vs2, ts2[:], lst2, 0, S)
-        gather(vw[0], tw[0][:].bitcast(U32), lst, 0, S)
-        gather(vs, ts[:], lst, 0, S)
-        gather(vw[1], tw[1][:].bitcast(U32), lst, 0, S)
-        displacement(0, 0, 256)
-        influence(0, 0, ((EARLY, PACK), (0, EARLY)))
-        gather(vw[2], tw[2][:].bitcast(U32), lst2, 256, S)
+        gather(v2_scale, v2_table_scales[:], idx2, 0, S)
+        gather(picked_words[0], table_words[0][:].bitcast(U32), idx, 0, S)
+        gather(v_scale, v_table_scales[:], idx, 0, S)
+        gather(picked_words[1], table_words[1][:].bitcast(U32), idx, 0, S)
+
+        scalar_step(0, 0, step_tile())
+        gather(picked_words[2], table_words[2][:].bitcast(U32), idx2, STEP, S - STEP)
         for t in range(EARLY):
-            gather(gg[:, t, :], g[t][:], lst, 0, S)
-        displacement(0, 256, 256)
-        influence(0, 256, ((EARLY, PACK), (0, EARLY)))
-        displacement(0, 512, 256)
-        cast_a(0, 1, "SSSS")
-        influence(0, 512, ((EARLY, PACK), (0, EARLY)))
-        quant_a(0, 1)
-        cast_a(1, 1, "VVVV")
-        quant_a(1, 1)
-        displacement(0, 768, 256)
-        influence(0, 768, ((EARLY, PACK), (0, EARLY)))
-        for n_lo in range(0, S, 256):
-            for t in range(EARLY, PACK):
-                stiffness(0, n_lo, t, 0, 256)
-            for off in (0, BK):
-                stiffness_early(n_lo, off, BK)
-            for off in (0, BK):
-                response(0, n_lo, off)
-            for off in (0, BK):
-                quant_h(0, n_lo, off, BK)
-        for n_lo in (0, 256):
-            displacement(1, n_lo, 256)
-            influence(1, n_lo, ((0, 2), (2, PACK)))
-        cast_w(0, "S", 4)
-        cast_w(1, "V", 1)
-        displacement(1, 512, 512)
-        influence(1, 512, [(t, t + 1) for t in range(PACK)])
-        for n_lo in (0, 256):
-            for t in range(3):
-                stiffness(1, n_lo, t, 0, 256)
-            for off in (0, BK):
-                stiffness(1, n_lo, 3, off, BK)
-            for off in (0, BK):
-                response(1, n_lo, off)
-            for off in (0, BK):
-                quant_h(1, n_lo, off, BK)
-        quant_w()
-        forces(0, 512, "SSSo")
-        for t in (0, 1, 2):
-            stiffness(1, 512, t, 0, 512)
-        stiffness(1, 512, 3, 0, 256)
-        stiffness(1, 512, 3, 256, 256)
-        for off in (0, BK, 2 * BK):
-            response(1, 512, off)
-        quant_h(1, 512, 0, 256)
-        response(1, 512, 3 * BK)
-        quant_h(1, 512, 256, BK)
-        quant_h(1, 512, 384, BK)
-        forces(512, 256, "SSSo")
-        forces(768, 128, "SVVx")
-        forces(896, 128, "VSVx")
+            gather(g_early[:, t, :], g_table[t][:], idx, 0, S)
+        scalar_step(0, STEP, step_tile())
+        squares = displacement(0, 2 * STEP, step_tile())
+        rounded_01 = round_a(a_01, PACK)
+        invert(0, 2 * STEP, squares, spare([P, PACK, STEP], "third_influence"))
+        quantise_a(0, 1, rounded_01)
+        quantise_a(1, 1, round_a(a_11, 0))
+        scalar_step(0, 3 * STEP, spare([P, PACK, STEP], "fourth_influence"))
+        for first in STEPS:
+            vector_step(0, first)
+
+        for first in STEPS:
+            if first == 2 * STEP:
+                round_w(0, w_in[0])
+                round_w(1, w_in[1])
+            if first == STEP:
+                scalar_step(1, first, held([P, PACK, STEP], F32, "influence_before_w", "g_table0"))
+            else:
+                scalar_step(1, first, step_tile())
+        vector_step(1, 0)
+        vector_step(1, STEP)
+        w_codes = quantise_w("g_table0")
+        forces(w_codes, 0, 2 * STEP, ())
+        vector_step(1, 2 * STEP)
+        forces(w_codes, 2 * STEP, STEP, ())
+        vector_step(1, 3 * STEP)
+        forces(w_codes, 3 * STEP, BANK, (2,))
+        forces(w_codes, 3 * STEP + BANK, BANK, (0, 2))

@@ -63,12 +63,10 @@ def tile_list_mesh_contact_forces_kernel(
         h_scale = [held([P, S], U8, "h_scale%d" % i) for i in range(2)]
         g_early = held([P, EARLY, S], F32, "g_early")
         one = held([P, 1], F32, "one")
-        warm = held([P, 1], F32, "warm")
 
         for scales in (v2_table_scales, v_table_scales, b4_scales_in):
             nc.vector.memset(scales[:].bitcast(I32), 0)
         nc.gpsimd.memset(one[:], 1.0)
-        nc.scalar.activation(out=warm[:], in_=one[:], func=ACT.Abs_reciprocal_sqrt, bias=one[:])
 
         def load_words(i):
             src = tab_words[i] if i < 2 else tab2_words[0]

@@ -296,8 +296,8 @@ def tile_list_mesh_contact_forces_kernel(
         rounded_10 = round_a(a_10, PACK // 2)
         a_01 = load_a(0, 1)
         a_11 = load_a(1, 1)
-        w_in = [load_w(0), load_w(1)]
         load_g(1)
+        w_in = [load_w(0), load_w(1)]
 
         quantise_a(0, 0, rounded_00)
         quantise_a(1, 0, rounded_10)

@@ -40,8 +40,8 @@ def tile_list_mesh_contact_forces_kernel(
         def held(shape, dtype, name, tag=None):
             return keep.tile(shape, dtype, name=name, tag=tag or name, align_bytes=64)
 
-        def spare(shape, name):
-            return ring.tile(shape, F32, name=name, tag="spare", bufs=2)
+        def spare(shape, name, n):
+            return held(shape, F32, name, "spare%d" % n)
 
         idx = keep.tile([P, S // LIST_ROWS], U16, name="idx")
         idx2 = keep.tile([P, S // LIST_ROWS], U16, name="idx2")
@@ -55,7 +55,7 @@ def tile_list_mesh_contact_forces_kernel(
         picked_words = [held([P, S], U32, "picked_words%d" % i) for i in range(3)]
         v_scale = held([P, S], U8, "v_scale")
         v2_scale = held([P, S], U8, "v2_scale")
-        a_codes = [held([P, H], U32, "a_codes%d" % i) for i in range(2)]
+        a_codes = {}
         a_scale = [held([P, H], U8, "a_scale%d" % i) for i in range(2)]
         g_table = [held([P, T], F32, "g_table%d" % i) for i in range(2 * PACK)]
         w_scale = held([P, 2 * N], U8, "w_scale")
@@ -67,6 +67,8 @@ def tile_list_mesh_contact_forces_kernel(
         for scales in (v2_table_scales, v_table_scales, b4_scales_in):
             nc.vector.memset(scales[:].bitcast(I32), 0)
         nc.gpsimd.memset(one[:], 1.0)
+        warm = held([P, 1], F32, "warm")
+        nc.scalar.activation(out=warm[:], in_=one[:], func=ACT.Abs_reciprocal_sqrt)
 
         def load_words(i):
             src = tab_words[i] if i < 2 else tab2_words[0]
@@ -84,7 +86,7 @@ def tile_list_mesh_contact_forces_kernel(
                 )
 
         def load_a(n, half):
-            quarter = spare([P, PACK, PASS], "a_in")
+            quarter = spare([P, PACK, PASS], "a_in", n)
             src = a[n * PASS : (n + 1) * PASS, half * PASS : (half + 1) * PASS]
             nc.sync.dma_start(out=quarter[:], in_=src.rearrange("(p j) c -> p j c", j=PACK))
             return quarter
@@ -108,18 +110,19 @@ def tile_list_mesh_contact_forces_kernel(
             else:
                 nc.scalar.activation(out=dst, in_=src, func=ACT.Copy, scale=-1.0)
 
-        def round_a(quarter, planes_on_scalar):
-            rounded = ring.tile([P, PACK, P, PACK], BF16, name="a_rounded", bufs=2, align_bytes=64)
+        def round_a(n, quarter, planes_on_scalar):
+            rounded = held([P, PACK, P, PACK], BF16, "a_rounded", "rounded%d" % n)
             dst = rounded[:].rearrange("p t (q s) j -> p t q j s", s=RUN)
             src = quarter[:].rearrange("p j (q t s) -> p t q j s", t=PACK, s=RUN)
             for t in range(PACK):
                 negate(t >= planes_on_scalar, dst[:, t], src[:, t])
             return rounded
 
-        def quantise_a(n, half, rounded):
+        def quantise_a(n, half, rounded, tag=None):
             cols = slice(half * PASS, (half + 1) * PASS)
+            a_codes[n, half] = held([P, PASS], U32, "a_codes%d%d" % (n, half), tag)
             nc.vector.quantize_mx(
-                out=a_codes[n][:, cols].bitcast(FP8X4),
+                out=a_codes[n, half][:].bitcast(FP8X4),
                 scales=a_scale[n][:, cols],
                 in_=rounded[:].rearrange("p t m j -> p (t m j)"),
             )
@@ -132,7 +135,7 @@ def tile_list_mesh_contact_forces_kernel(
             width = N // RUN // W_PIECES
             for piece in range(W_PIECES):
                 part = slice(piece * width, (piece + 1) * width)
-                negate((half, piece) == (1, W_PIECES - 1), dst[:, part], src[:, part])
+                negate(W_PIECES * half + piece >= 8, dst[:, part], src[:, part])
 
         def quantise_w(tag):
             w_codes = held([P, 2 * N], U32, "w_codes", tag)
@@ -161,23 +164,19 @@ def tile_list_mesh_contact_forces_kernel(
             nc.vector.tensor_copy(out=dst[:, first : first + count], in_=table.indirect(entries(lst, first, count)))
 
         banks = {}
-        influence = {}
-
-        def step_tile():
-            return ring.tile([P, PACK, STEP], F32, name="squares", bufs=3)
 
         def displacement(half, first, squares):
-            for n0 in range(first, first + STEP, BANK):
+            for off in range(0, squares[:].shape[2], BANK):
                 bank = psum.tile([P, PACK, BANK], F32, name="bank", bufs=8)
-                banks[half, n0] = bank
-                cols = slice(n0, n0 + BANK)
+                banks[half, first + off] = bank
+                cols = slice(first + off, first + off + BANK)
                 for t in range(PACK):
                     m0 = half * PASS + t * P
                     rows = slice(m0, m0 + P)
                     for n in range(2):
                         nc.tensor.matmul_mx(
                             out=bank[:, t, :],
-                            lhsT=a_codes[n][:, rows].bitcast(FP8X4),
+                            lhsT=a_codes[n, half][:, t * P : (t + 1) * P].bitcast(FP8X4),
                             lhsT_scale=a_scale[n][:, rows],
                             rhs=picked_words[n][:, cols].bitcast(FP8X4),
                             rhs_scale=v_scale[4 + 4 * n :, cols],
@@ -193,51 +192,52 @@ def tile_list_mesh_contact_forces_kernel(
                         start=False,
                         stop=True,
                     )
-                nc.scalar.activation(out=squares[:, :, n0 - first : n0 - first + BANK], in_=bank[:], func=ACT.Square)
+                nc.scalar.activation(out=squares[:, :, off : off + BANK], in_=bank[:], func=ACT.Square)
             return squares
 
-        def invert(half, first, squares, result):
-            influence[half, first] = result
-            groups = (slice(EARLY, PACK), slice(0, EARLY)) if half == 0 else (slice(0, 2), slice(2, PACK))
-            for planes in groups:
-                nc.scalar.activation(
-                    out=result[:, planes, :], in_=squares[:, planes, :], func=ACT.Abs_reciprocal_sqrt, bias=one[:]
-                )
-            for planes in groups:
-                nc.scalar.activation(out=result[:, planes, :], in_=result[:, planes, :], func=ACT.Square)
+        def invert(half, squares, influence):
+            planes = PASS // squares[:].shape[2]
+            starts = [(t + (EARLY if half == 0 else 0)) % PACK for t in range(0, PACK, planes)]
+            for two in range(0, len(starts), 2):
+                pieces = [slice(t, t + planes) for t in starts[two : two + 2]]
+                for piece in pieces:
+                    nc.scalar.activation(
+                        out=influence[:, piece, :], in_=squares[:, piece, :], func=ACT.Abs_reciprocal_sqrt, bias=one[:]
+                    )
+                for piece in pieces:
+                    nc.scalar.activation(out=influence[:, piece, :], in_=influence[:, piece, :], func=ACT.Square)
+            return influence
 
         def scalar_step(half, first, tile):
-            invert(half, first, displacement(half, first, tile), tile)
+            return invert(half, displacement(half, first, tile), tile)
 
-        def vector_step(half, first):
-            weight = ring.tile([P, PACK, STEP], F32, name="weight", bufs=1, align_bytes=64)
-            infl = influence[half, first]
+        def vector_step(half, first, influence, tag="weight"):
+            count = influence[:].shape[2]
+            weight = held([P, PACK, count], F32, "weight", tag)
+            halves = (slice(0, count // 2), slice(count // 2, count))
 
-            def gather_times_influence(t, off, count):
+            def gather_times_influence(t, part):
                 nc.vector.tensor_tensor(
-                    out=weight[:, t, off : off + count],
-                    in0=g_table[PACK * half + t][:].indirect(entries(idx, first + off, count)),
-                    in1=infl[:, t, off : off + count],
+                    out=weight[:, t, part],
+                    in0=g_table[PACK * half + t][:].indirect(entries(idx, first + part.start, part.stop - part.start)),
+                    in1=influence[:, t, part],
                     op=MULT,
                 )
 
-            if half == 0:
-                for t in range(EARLY, PACK):
-                    gather_times_influence(t, 0, STEP)
-                for off in (0, BANK):
-                    nc.vector.tensor_tensor(
-                        out=weight[:, 0:EARLY, off : off + BANK],
-                        in0=g_early[:, :, first + off : first + off + BANK],
-                        in1=infl[:, 0:EARLY, off : off + BANK],
-                        op=MULT,
-                    )
-            else:
-                for t in range(PACK - 1):
-                    gather_times_influence(t, 0, STEP)
-                for off in (0, BANK):
-                    gather_times_influence(PACK - 1, off, BANK)
-            h_rounded = ring.tile([P, STEP, PACK], BF16, name="h_rounded", bufs=2, align_bytes=64)
-            for off in (0, BANK):
+            early = EARLY if half == 0 else 0
+            for t in range(early, PACK - 1):
+                gather_times_influence(t, slice(0, count))
+            for part in halves if early == 0 or first == 0 else (slice(0, count),):
+                gather_times_influence(PACK - 1, part)
+            for part in halves if early else ():
+                nc.vector.tensor_tensor(
+                    out=weight[:, 0:early, part],
+                    in0=g_early[:, :, first + part.start : first + part.stop],
+                    in1=influence[:, 0:early, part],
+                    op=MULT,
+                )
+            h_rounded = ring.tile([P, count, PACK], BF16, name="h_rounded", bufs=2, align_bytes=64)
+            for off in range(0, count, BANK):
                 cols = slice(off, off + BANK)
                 nc.vector.tensor_tensor(
                     out=h_rounded[:, cols, :].rearrange("p (c i) t -> p c t i", i=RUN),
@@ -245,20 +245,22 @@ def tile_list_mesh_contact_forces_kernel(
                     in1=weight[:, :, cols].rearrange("p t (c i) -> p c t i", i=RUN),
                     op=MULT,
                 )
-            for off in (0, BANK):
-                cols = slice(first + off, first + off + BANK)
+            for part in halves:
+                cols = slice(first + part.start, first + part.stop)
                 nc.vector.quantize_mx(
                     out=h_codes[half][:, cols].bitcast(FP8X4),
                     scales=h_scale[half][:, cols],
-                    in_=h_rounded[:, off : off + BANK, :].rearrange("p n t -> p (n t)"),
+                    in_=h_rounded[:, part, :].rearrange("p n t -> p (n t)"),
                 )
 
         out_rows = out.rearrange("(c p) j -> p c j", p=P)
 
         def forces(w_codes, first, count, blocks_on_vector):
             cols = slice(first, first + count)
-            if count > BANK:
-                stage = spare([P, N // P, count], "wide_stage")
+            if first == 0:
+                stage = held([P, N // P, count], F32, "first_stage", "last_squares")
+            elif count > BANK:
+                stage = spare([P, N // P, count], "wide_stage", 0)
             else:
                 stage = ring.tile([P, N // P, count], F32, name="stage", bufs=2)
             for c in range(N // P):
@@ -278,7 +280,10 @@ def tile_list_mesh_contact_forces_kernel(
                     nc.vector.tensor_copy(out=stage[:, c, :], in_=acc[:])
                 else:
                     nc.scalar.copy(out=stage[:, c, :], in_=acc[:])
-            nc.sync.dma_start(out=out_rows[:, :, cols], in_=stage[:])
+                if first == 0:
+                    nc.sync.dma_start(out=out_rows[:, c, cols], in_=stage[:, c, :])
+            if first > 0:
+                nc.sync.dma_start(out=out_rows[:, :, cols], in_=stage[:])
 
         nc.sync.dma_start(idx2[:], offs2)
         nc.sync.dma_start(idx[:], offs)
@@ -292,14 +297,13 @@ def tile_list_mesh_contact_forces_kernel(
         nc.sync.dma_start(out=b4_words_in[:].bitcast(I32), in_=b4_words[0].bitcast(I32))
         load_words(2)
         load_g(0)
-        rounded_00 = round_a(a_00, PACK)
-        rounded_10 = round_a(a_10, PACK // 2)
+        rounded_00 = round_a(0, a_00, PACK)
+        rounded_10 = round_a(1, a_10, PACK // 2)
         a_01 = load_a(0, 1)
         a_11 = load_a(1, 1)
         load_g(1)
-        w_in = [load_w(0), load_w(1)]
 
-        quantise_a(0, 0, rounded_00)
+        quantise_a(0, 0, rounded_00, "table_words1")
         quantise_a(1, 0, rounded_10)
         gather(picked_words[2], table_words[2][:].bitcast(U32), idx2, 0, STEP)
         deal_b4()
@@ -308,34 +312,34 @@ def tile_list_mesh_contact_forces_kernel(
         gather(v_scale, v_table_scales[:], idx, 0, S)
         gather(picked_words[1], table_words[1][:].bitcast(U32), idx, 0, S)
 
-        scalar_step(0, 0, step_tile())
+        w_in = [load_w(0), load_w(1)]
+
+        first_influence = scalar_step(0, 0, held([P, PACK, STEP], F32, "first_influence"))
         gather(picked_words[2], table_words[2][:].bitcast(U32), idx2, STEP, S - STEP)
         for t in range(EARLY):
             gather(g_early[:, t, :], g_table[t][:], idx, 0, S)
-        scalar_step(0, STEP, step_tile())
-        squares = displacement(0, 2 * STEP, step_tile())
-        rounded_01 = round_a(a_01, PACK)
-        invert(0, 2 * STEP, squares, spare([P, PACK, STEP], "third_influence"))
-        quantise_a(0, 1, rounded_01)
-        quantise_a(1, 1, round_a(a_11, 0))
-        scalar_step(0, 3 * STEP, spare([P, PACK, STEP], "fourth_influence"))
-        for first in STEPS:
-            vector_step(0, first)
+        second_influence = scalar_step(0, STEP, held([P, PACK, STEP], F32, "second_influence"))
+        squares = displacement(0, 2 * STEP, held([P, PACK, 2 * STEP], F32, "wide_squares"))
+        rounded_01 = round_a(0, a_01, PACK)
+        third_influence = invert(0, squares, spare([P, PACK, 2 * STEP], "third_influence", 0))
+        rounded_11 = round_a(1, a_11, 0)
+        quantise_a(0, 1, rounded_01, "spare1")
+        quantise_a(1, 1, rounded_11)
+        vector_step(0, 0, first_influence)
+        vector_step(0, STEP, second_influence)
+        vector_step(0, 2 * STEP, third_influence, "rounded1")
 
-        for first in STEPS:
-            if first == 2 * STEP:
-                round_w(0, w_in[0])
-                round_w(1, w_in[1])
-            if first == STEP:
-                scalar_step(1, first, held([P, PACK, STEP], F32, "influence_before_w", "g_table0"))
-            else:
-                scalar_step(1, first, step_tile())
-        vector_step(1, 0)
-        vector_step(1, STEP)
+        fourth_influence = scalar_step(1, 0, held([P, PACK, STEP], F32, "fourth_influence", "first_influence"))
+        fifth_influence = scalar_step(1, STEP, held([P, PACK, 2 * STEP], F32, "fifth_influence", "g_table0"))
+        squares = displacement(1, 3 * STEP, held([P, PACK, STEP], F32, "last_squares"))
+        round_w(0, w_in[0])
+        round_w(1, w_in[1])
+        last_influence = invert(1, squares, held([P, PACK, STEP], F32, "last_influence", "table_words0"))
+        vector_step(1, 0, fourth_influence)
+        vector_step(1, STEP, fifth_influence)
         w_codes = quantise_w("g_table0")
         forces(w_codes, 0, 2 * STEP, ())
-        vector_step(1, 2 * STEP)
         forces(w_codes, 2 * STEP, STEP, ())
-        vector_step(1, 3 * STEP)
+        vector_step(1, 3 * STEP, last_influence)
         forces(w_codes, 3 * STEP, BANK, (2,))
         forces(w_codes, 3 * STEP + BANK, BANK, (0, 2))

@@ -78,11 +78,10 @@ def tile_list_mesh_contact_forces_kernel(
             for r in range(4):
                 nc.sync.dma_start(out=scales[r:P:32, :].bitcast(I32), in_=src[0, r:16:4, :].bitcast(I32))
 
-        def load_v_scales():
-            for quad in range(4):
+        def load_v_scales(n):
+            for r in range(4):
                 nc.sync.dma_start(
-                    out=v_table_scales[32 * quad + 4 : 32 * quad + 12, :].bitcast(I32),
-                    in_=tab_scales[:, 4 * quad : 4 * quad + 4, :].bitcast(I32),
+                    out=v_table_scales[4 + 4 * n + r : P : 32, :].bitcast(I32), in_=tab_scales[n, r:16:4, :].bitcast(I32)
                 )
 
         def load_a(n, half):
@@ -170,27 +169,25 @@ def tile_list_mesh_contact_forces_kernel(
                 bank = psum.tile([P, PACK, BANK], F32, name="bank", bufs=8)
                 banks[half, first + off] = bank
                 cols = slice(first + off, first + off + BANK)
-                for t in range(PACK):
+                passes = [(t, n) for t in range(PACK) for n in range(3)]
+                one_group = half == 0 and first == 0
+                if one_group:
+                    passes = [(t, n) for n in range(3) for t in range(PACK)]
+                for t, n in passes:
                     m0 = half * PASS + t * P
-                    rows = slice(m0, m0 + P)
-                    for n in range(2):
-                        nc.tensor.matmul_mx(
-                            out=bank[:, t, :],
-                            lhsT=a_codes[n, half][:, t * P : (t + 1) * P].bitcast(FP8X4),
-                            lhsT_scale=a_scale[n][:, rows],
-                            rhs=picked_words[n][:, cols].bitcast(FP8X4),
-                            rhs_scale=v_scale[4 + 4 * n :, cols],
-                            start=(n == 0),
-                            stop=False,
-                        )
+                    with_a = n < 2
                     nc.tensor.matmul_mx(
                         out=bank[:, t, :],
-                        lhsT=b4_codes[:, 2 * m0 : 2 * (m0 + P)].bitcast(FP4X4),
-                        lhsT_scale=b4_scale[:, rows],
-                        rhs=picked_words[2][:, cols].bitcast(FP8X4),
-                        rhs_scale=v2_scale[:, cols],
-                        start=False,
-                        stop=True,
+                        lhsT=(
+                            a_codes[n, half][:, t * P : (t + 1) * P].bitcast(FP8X4)
+                            if with_a
+                            else b4_codes[:, 2 * m0 : 2 * (m0 + P)].bitcast(FP4X4)
+                        ),
+                        lhsT_scale=(a_scale[n] if with_a else b4_scale)[:, m0 : m0 + P],
+                        rhs=picked_words[n][:, cols].bitcast(FP8X4),
+                        rhs_scale=v_scale[4 + 4 * n :, cols] if with_a else v2_scale[:, cols],
+                        start=(n == 0 and (t == 0 or not one_group)),
+                        stop=(n == 2 and (t == PACK - 1 or not one_group)),
                     )
                 nc.scalar.activation(out=squares[:, :, off : off + BANK], in_=bank[:], func=ACT.Square)
             return squares
@@ -286,15 +283,16 @@ def tile_list_mesh_contact_forces_kernel(
                 nc.sync.dma_start(out=out_rows[:, :, cols], in_=stage[:])
 
         nc.sync.dma_start(idx2[:], offs2)
+        nc.sync.dma_start(out=b4_words_in[:].bitcast(I32), in_=b4_words[0].bitcast(I32))
         nc.sync.dma_start(idx[:], offs)
         load_scales(v2_table_scales, tab2_scales)
         load_words(0)
-        load_v_scales()
+        load_v_scales(0)
         a_00 = load_a(0, 0)
+        load_v_scales(1)
         load_words(1)
         a_10 = load_a(1, 0)
         load_scales(b4_scales_in, b4_scales)
-        nc.sync.dma_start(out=b4_words_in[:].bitcast(I32), in_=b4_words[0].bitcast(I32))
         load_words(2)
         load_g(0)
         rounded_00 = round_a(0, a_00, PACK)
@@ -306,6 +304,7 @@ def tile_list_mesh_contact_forces_kernel(
         quantise_a(0, 0, rounded_00, "table_words1")
         quantise_a(1, 0, rounded_10)
         gather(picked_words[2], table_words[2][:].bitcast(U32), idx2, 0, STEP)
+        gather(picked_words[2], table_words[2][:].bitcast(U32), idx2, STEP, STEP)
         deal_b4()
         gather(v2_scale, v2_table_scales[:], idx2, 0, S)
         gather(picked_words[0], table_words[0][:].bitcast(U32), idx, 0, S)
@@ -315,7 +314,7 @@ def tile_list_mesh_contact_forces_kernel(
         w_in = [load_w(0), load_w(1)]
 
         first_influence = scalar_step(0, 0, held([P, PACK, STEP], F32, "first_influence"))
-        gather(picked_words[2], table_words[2][:].bitcast(U32), idx2, STEP, S - STEP)
+        gather(picked_words[2], table_words[2][:].bitcast(U32), idx2, 2 * STEP, S - 2 * STEP)
         for t in range(EARLY):
             gather(g_early[:, t, :], g_table[t][:], idx, 0, S)
         second_influence = scalar_step(0, STEP, held([P, PACK, STEP], F32, "second_influence"))

@@ -25,7 +25,6 @@ STEP = 2 * BANK
 STEPS = range(0, S, STEP)
 LIST_ROWS = 16
 EARLY = 2
-W_PIECES = 4
 
 
 def tile_list_mesh_contact_forces_kernel(
@@ -128,13 +127,11 @@ def tile_list_mesh_contact_forces_kernel(
 
         w_rounded = held([P, 2 * N * PACK], BF16, "w_rounded")
 
-        def round_w(half, w_in):
-            dst = w_rounded[:, half * N * PACK : (half + 1) * N * PACK].rearrange("p (c i t) -> p c t i", i=RUN, t=PACK)
-            src = w_in[:].rearrange("p t (c i) -> p c t i", i=RUN)
-            width = N // RUN // W_PIECES
-            for piece in range(W_PIECES):
-                part = slice(piece * width, (piece + 1) * width)
-                negate(W_PIECES * half + piece >= 8, dst[:, part], src[:, part])
+        def round_w(c, half, w_in):
+            w0 = (2 * c + half) * P * PACK
+            dst = w_rounded[:, w0 : w0 + P * PACK].rearrange("p (c i t) -> p c t i", i=RUN, t=PACK)
+            src = w_in[half][:, :, c * P : (c + 1) * P].rearrange("p t (c i) -> p c t i", i=RUN)
+            negate(False, dst, src)
 
         def quantise_w(tag):
             w_codes = held([P, 2 * N], U32, "w_codes", tag)
@@ -147,11 +144,12 @@ def tile_list_mesh_contact_forces_kernel(
             return w_codes
 
         def deal_b4():
-            nc.vector.tensor_copy(
-                out=b4_codes[:].bitcast(I32).rearrange("p (h t q e) -> p h t q e", h=2, t=PACK, e=2),
-                in_=b4_words_in[:].bitcast(I32).rearrange("p (h q t e) -> p h t q e", h=2, t=PACK, e=2),
-            )
-            nc.vector.tensor_copy(
+            for h in range(2):
+                nc.gpsimd.tensor_copy(
+                    out=b4_codes[:].bitcast(I32).rearrange("p (h t q e) -> p h t q e", h=2, t=PACK, e=2)[:, h],
+                    in_=b4_words_in[:].bitcast(I32).rearrange("p (h q t e) -> p h t q e", h=2, t=PACK, e=2)[:, h],
+                )
+            nc.gpsimd.tensor_copy(
                 out=b4_scale[:].bitcast(I32).rearrange("p (h t q) -> p h t q", h=2, t=PACK),
                 in_=b4_scales_in[:].bitcast(I32).rearrange("p (h q t) -> p h t q", h=2, t=PACK),
             )
@@ -170,9 +168,9 @@ def tile_list_mesh_contact_forces_kernel(
                 banks[half, first + off] = bank
                 cols = slice(first + off, first + off + BANK)
                 passes = [(t, n) for t in range(PACK) for n in range(3)]
-                one_group = half == 0 and first == 0
+                one_group = half == 1 or first == 0
                 if one_group:
-                    passes = [(t, n) for n in range(3) for t in range(PACK)]
+                    passes = [(t, n) for n in ((0, 1, 2) if half == 0 else (2, 0, 1)) for t in range(PACK)]
                 for t, n in passes:
                     m0 = half * PASS + t * P
                     with_a = n < 2
@@ -186,8 +184,8 @@ def tile_list_mesh_contact_forces_kernel(
                         lhsT_scale=(a_scale[n] if with_a else b4_scale)[:, m0 : m0 + P],
                         rhs=picked_words[n][:, cols].bitcast(FP8X4),
                         rhs_scale=v_scale[4 + 4 * n :, cols] if with_a else v2_scale[:, cols],
-                        start=(n == 0 and (t == 0 or not one_group)),
-                        stop=(n == 2 and (t == PACK - 1 or not one_group)),
+                        start=((t, n) == passes[0] if one_group else n == 0),
+                        stop=((t, n) == passes[-1] if one_group else n == 2),
                     )
                 nc.scalar.activation(out=squares[:, :, off : off + BANK], in_=bank[:], func=ACT.Square)
             return squares
@@ -208,7 +206,7 @@ def tile_list_mesh_contact_forces_kernel(
         def scalar_step(half, first, tile):
             return invert(half, displacement(half, first, tile), tile)
 
-        def vector_step(half, first, influence, tag="weight"):
+        def vector_step(half, first, influence, tag="weight", between=None):
             count = influence[:].shape[2]
             weight = held([P, PACK, count], F32, "weight", tag)
             halves = (slice(0, count // 2), slice(count // 2, count))
@@ -242,6 +240,8 @@ def tile_list_mesh_contact_forces_kernel(
                     in1=weight[:, :, cols].rearrange("p t (c i) -> p c t i", i=RUN),
                     op=MULT,
                 )
+            if between is not None:
+                between()
             for part in halves:
                 cols = slice(first + part.start, first + part.stop)
                 nc.vector.quantize_mx(
@@ -263,7 +263,7 @@ def tile_list_mesh_contact_forces_kernel(
             for c in range(N // P):
                 acc = psum.tile([P, count], F32, name="bank", bufs=8)
                 for half in range(2):
-                    rows = slice(half * N + c * P, half * N + (c + 1) * P)
+                    rows = slice((2 * c + half) * P, (2 * c + half + 1) * P)
                     nc.tensor.matmul_mx(
                         out=acc[:],
                         lhsT=w_codes[:, rows].bitcast(FP8X4),
@@ -277,9 +277,9 @@ def tile_list_mesh_contact_forces_kernel(
                     nc.vector.tensor_copy(out=stage[:, c, :], in_=acc[:])
                 else:
                     nc.scalar.copy(out=stage[:, c, :], in_=acc[:])
-                if first == 0:
+                if count > BANK:
                     nc.sync.dma_start(out=out_rows[:, c, cols], in_=stage[:, c, :])
-            if first > 0:
+            if count == BANK:
                 nc.sync.dma_start(out=out_rows[:, :, cols], in_=stage[:])
 
         nc.sync.dma_start(idx2[:], offs2)
@@ -320,25 +320,29 @@ def tile_list_mesh_contact_forces_kernel(
         second_influence = scalar_step(0, STEP, held([P, PACK, STEP], F32, "second_influence"))
         squares = displacement(0, 2 * STEP, held([P, PACK, 2 * STEP], F32, "wide_squares"))
         rounded_01 = round_a(0, a_01, PACK)
-        third_influence = invert(0, squares, spare([P, PACK, 2 * STEP], "third_influence", 0))
         rounded_11 = round_a(1, a_11, 0)
+        third_influence = invert(0, squares, spare([P, PACK, 2 * STEP], "third_influence", 0))
         quantise_a(0, 1, rounded_01, "spare1")
         quantise_a(1, 1, rounded_11)
         vector_step(0, 0, first_influence)
         vector_step(0, STEP, second_influence)
-        vector_step(0, 2 * STEP, third_influence, "rounded1")
+        vector_step(0, 2 * STEP, third_influence)
 
         fourth_influence = scalar_step(1, 0, held([P, PACK, STEP], F32, "fourth_influence", "first_influence"))
         fifth_influence = scalar_step(1, STEP, held([P, PACK, 2 * STEP], F32, "fifth_influence", "g_table0"))
+        for half in range(2):
+            for c in range(2):
+                round_w(c, half, w_in)
+        round_w(2, 0, w_in)
         squares = displacement(1, 3 * STEP, held([P, PACK, STEP], F32, "last_squares"))
-        round_w(0, w_in[0])
-        round_w(1, w_in[1])
+        round_w(2, 1, w_in)
         last_influence = invert(1, squares, held([P, PACK, STEP], F32, "last_influence", "table_words0"))
         vector_step(1, 0, fourth_influence)
-        vector_step(1, STEP, fifth_influence)
-        w_codes = quantise_w("g_table0")
-        forces(w_codes, 0, 2 * STEP, ())
-        forces(w_codes, 2 * STEP, STEP, ())
+        made = []
+        vector_step(1, STEP, fifth_influence, between=lambda: made.append(quantise_w("g_table0")))
+        w_codes = made[0]
+        forces(w_codes, 0, STEP, ())
+        forces(w_codes, STEP, 2 * STEP, ())
         vector_step(1, 3 * STEP, last_influence)
         forces(w_codes, 3 * STEP, BANK, (2,))
         forces(w_codes, 3 * STEP + BANK, BANK, (0, 2))

@@ -64,7 +64,7 @@ def tile_list_mesh_contact_forces_kernel(
         one = held([P, 1], F32, "one")
 
         for scales in (v2_table_scales, v_table_scales, b4_scales_in):
-            nc.vector.memset(scales[:].bitcast(I32), 0)
+            nc.gpsimd.memset(scales[:].bitcast(I32), 0)
         nc.gpsimd.memset(one[:], 1.0)
         warm = held([P, 1], F32, "warm")
         nc.scalar.activation(out=warm[:], in_=one[:], func=ACT.Abs_reciprocal_sqrt)
@@ -288,9 +288,9 @@ def tile_list_mesh_contact_forces_kernel(
         load_scales(v2_table_scales, tab2_scales)
         load_words(0)
         load_v_scales(0)
-        a_00 = load_a(0, 0)
-        load_v_scales(1)
         load_words(1)
+        load_v_scales(1)
+        a_00 = load_a(0, 0)
         a_10 = load_a(1, 0)
         load_scales(b4_scales_in, b4_scales)
         load_words(2)
@@ -301,7 +301,7 @@ def tile_list_mesh_contact_forces_kernel(
         a_11 = load_a(1, 1)
         load_g(1)
 
-        quantise_a(0, 0, rounded_00, "table_words1")
+        quantise_a(0, 0, rounded_00)
         quantise_a(1, 0, rounded_10)
         gather(picked_words[2], table_words[2][:].bitcast(U32), idx2, 0, STEP)
         gather(picked_words[2], table_words[2][:].bitcast(U32), idx2, STEP, STEP)

@@ -73,8 +73,8 @@ def tile_list_mesh_contact_forces_kernel(
             src = tab_words[i] if i < 2 else tab2_words[0]
             nc.sync.dma_start(out=table_words[i][:], in_=src.rearrange("p t i -> p (t i)").bitcast(I32))
 
-        def load_scales(scales, src):
-            for r in range(4):
+        def load_scales(scales, src, rows=range(4)):
+            for r in rows:
                 nc.sync.dma_start(out=scales[r:P:32, :].bitcast(I32), in_=src[0, r:16:4, :].bitcast(I32))
 
         def load_v_scales(n):
@@ -144,12 +144,11 @@ def tile_list_mesh_contact_forces_kernel(
             return w_codes
 
         def deal_b4():
-            for h in range(2):
-                nc.gpsimd.tensor_copy(
-                    out=b4_codes[:].bitcast(I32).rearrange("p (h t q e) -> p h t q e", h=2, t=PACK, e=2)[:, h],
-                    in_=b4_words_in[:].bitcast(I32).rearrange("p (h q t e) -> p h t q e", h=2, t=PACK, e=2)[:, h],
-                )
-            nc.gpsimd.tensor_copy(
+            nc.vector.tensor_copy(
+                out=b4_codes[:].bitcast(I32).rearrange("p (h t q e) -> p h t q e", h=2, t=PACK, e=2),
+                in_=b4_words_in[:].bitcast(I32).rearrange("p (h q t e) -> p h t q e", h=2, t=PACK, e=2),
+            )
+            nc.vector.tensor_copy(
                 out=b4_scale[:].bitcast(I32).rearrange("p (h t q) -> p h t q", h=2, t=PACK),
                 in_=b4_scales_in[:].bitcast(I32).rearrange("p (h q t) -> p h t q", h=2, t=PACK),
             )
@@ -168,7 +167,7 @@ def tile_list_mesh_contact_forces_kernel(
                 banks[half, first + off] = bank
                 cols = slice(first + off, first + off + BANK)
                 passes = [(t, n) for t in range(PACK) for n in range(3)]
-                one_group = half == 1 or first == 0
+                one_group = half == 1 or first + off < STEP
                 if one_group:
                     passes = [(t, n) for n in ((0, 1, 2) if half == 0 else (2, 0, 1)) for t in range(PACK)]
                 for t, n in passes:
@@ -187,7 +186,7 @@ def tile_list_mesh_contact_forces_kernel(
                         start=((t, n) == passes[0] if one_group else n == 0),
                         stop=((t, n) == passes[-1] if one_group else n == 2),
                     )
-                nc.scalar.activation(out=squares[:, :, off : off + BANK], in_=bank[:], func=ACT.Square)
+                nc.scalar.activation(out=squares[:, 0:PACK, off : off + BANK], in_=bank[:], func=ACT.Square)
             return squares
 
         def invert(half, squares, influence):
@@ -208,7 +207,7 @@ def tile_list_mesh_contact_forces_kernel(
 
         def vector_step(half, first, influence, tag="weight", between=None):
             count = influence[:].shape[2]
-            weight = held([P, PACK, count], F32, "weight", tag)
+            weight = held([P, PACK, count], F32, "weight", tag)[:] if half == 1 else influence[:, EARLY:, :]
             halves = (slice(0, count // 2), slice(count // 2, count))
 
             def gather_times_influence(t, part):
@@ -222,7 +221,7 @@ def tile_list_mesh_contact_forces_kernel(
             early = EARLY if half == 0 else 0
             for t in range(early, PACK - 1):
                 gather_times_influence(t, slice(0, count))
-            for part in halves if early == 0 or first == 0 else (slice(0, count),):
+            for part in halves:
                 gather_times_influence(PACK - 1, part)
             for part in halves if early else ():
                 nc.vector.tensor_tensor(
@@ -254,6 +253,7 @@ def tile_list_mesh_contact_forces_kernel(
 
         def forces(w_codes, first, count, blocks_on_vector):
             cols = slice(first, first + count)
+            by_block = count > BANK or first + count == S
             if first == 0:
                 stage = held([P, N // P, count], F32, "first_stage", "last_squares")
             elif count > BANK:
@@ -277,9 +277,9 @@ def tile_list_mesh_contact_forces_kernel(
                     nc.vector.tensor_copy(out=stage[:, c, :], in_=acc[:])
                 else:
                     nc.scalar.copy(out=stage[:, c, :], in_=acc[:])
-                if count > BANK:
+                if by_block:
                     nc.sync.dma_start(out=out_rows[:, c, cols], in_=stage[:, c, :])
-            if count == BANK:
+            if not by_block:
                 nc.sync.dma_start(out=out_rows[:, :, cols], in_=stage[:])
 
         nc.sync.dma_start(idx2[:], offs2)
@@ -291,12 +291,13 @@ def tile_list_mesh_contact_forces_kernel(
         load_words(1)
         load_v_scales(1)
         a_00 = load_a(0, 0)
+        load_scales(b4_scales_in, b4_scales, range(3))
         a_10 = load_a(1, 0)
-        load_scales(b4_scales_in, b4_scales)
+        load_scales(b4_scales_in, b4_scales, range(3, 4))
         load_words(2)
         load_g(0)
         rounded_00 = round_a(0, a_00, PACK)
-        rounded_10 = round_a(1, a_10, PACK // 2)
+        rounded_10 = round_a(1, a_10, 3)
         a_01 = load_a(0, 1)
         a_11 = load_a(1, 1)
         load_g(1)
@@ -313,19 +314,17 @@ def tile_list_mesh_contact_forces_kernel(
 
         w_in = [load_w(0), load_w(1)]
 
-        first_influence = scalar_step(0, 0, held([P, PACK, STEP], F32, "first_influence"))
+        first_influence = scalar_step(0, 0, held([P, PACK + EARLY, 2 * STEP], F32, "first_influence"))
         gather(picked_words[2], table_words[2][:].bitcast(U32), idx2, 2 * STEP, S - 2 * STEP)
         for t in range(EARLY):
             gather(g_early[:, t, :], g_table[t][:], idx, 0, S)
-        second_influence = scalar_step(0, STEP, held([P, PACK, STEP], F32, "second_influence"))
         squares = displacement(0, 2 * STEP, held([P, PACK, 2 * STEP], F32, "wide_squares"))
         rounded_01 = round_a(0, a_01, PACK)
         rounded_11 = round_a(1, a_11, 0)
-        third_influence = invert(0, squares, spare([P, PACK, 2 * STEP], "third_influence", 0))
-        quantise_a(0, 1, rounded_01, "spare1")
+        third_influence = invert(0, squares, spare([P, PACK + EARLY, 2 * STEP], "third_influence", 0))
+        quantise_a(0, 1, rounded_01)
         quantise_a(1, 1, rounded_11)
         vector_step(0, 0, first_influence)
-        vector_step(0, STEP, second_influence)
         vector_step(0, 2 * STEP, third_influence)
 
         fourth_influence = scalar_step(1, 0, held([P, PACK, STEP], F32, "fourth_influence", "first_influence"))

from contextlib import ExitStack

import concourse.mybir as mybir

K, K2, H, N, T, S = 1024, 512, 1024, 384, 2048, 1024
FLOPS = 2 * S * (K * H + K2 * H + H * N)

F32 = mybir.dt.float32
BF16 = mybir.dt.bfloat16
I32 = mybir.dt.int32
U32 = mybir.dt.uint32
U16 = mybir.dt.uint16
U8 = mybir.dt.uint8
FP8X4 = mybir.dt.float8_e4m3fn_x4
FP4X4 = mybir.dt.float4_e2m1fn_x4
ACT = mybir.ActivationFunctionType
MULT = mybir.AluOpType.mult

P = 128
PACK = 4
PASS = P * PACK
RUN = 4
BANK = 128
STEP = 2 * BANK
STEPS = range(0, S, STEP)
LIST_ROWS = 16
EARLY = 2


def tile_list_mesh_contact_forces_kernel(
    tc, tab_words, tab_scales, tab2_words, tab2_scales, offs, offs2, a, b4_words, b4_scales, gT, w, out
):
    nc = tc.nc
    with ExitStack() as ctx:
        keep = ctx.enter_context(tc.tile_pool(name="keep", bufs=1))
        ring = ctx.enter_context(tc.tile_pool(name="ring", bufs=2))
        psum = ctx.enter_context(tc.psum_pool(name="psum", bufs=1))

        def held(shape, dtype, name, tag=None):
            return keep.tile(shape, dtype, name=name, tag=tag or name, align_bytes=64)

        def spare(shape, name, n):
            return held(shape, F32, name, "spare%d" % n)

        idx = keep.tile([P, S // LIST_ROWS], U16, name="idx")
        idx2 = keep.tile([P, S // LIST_ROWS], U16, name="idx2")
        table_words = [held([P, T], I32, "table_words%d" % i) for i in range(3)]
        v_table_scales = held([P, T], U8, "v_table_scales")
        v2_table_scales = held([P, T], U8, "v2_table_scales")
        b4_words_in = held([P, 2 * H], U8, "b4_words_in")
        b4_scales_in = held([P, H], U8, "b4_scales_in")
        b4_codes = held([P, 2 * H], U8, "b4_codes")
        b4_scale = held([P, H], U8, "b4_scale")
        picked_words = [held([P, S], U32, "picked_words%d" % i) for i in range(3)]
        v_scale = held([P, S], U8, "v_scale")
        v2_scale = held([P, S], U8, "v2_scale")
        a_codes = {}
        a_scale = [held([P, H], U8, "a_scale%d" % i) for i in range(2)]
        g_table = [held([P, T], F32, "g_table%d" % i) for i in range(2 * PACK)]
        w_scale = held([P, 2 * N], U8, "w_scale")
        h_codes = [held([P, S], U32, "h_codes%d" % i) for i in range(2)]
        h_scale = [held([P, S], U8, "h_scale%d" % i) for i in range(2)]
        g_early = held([P, EARLY, S], F32, "g_early")
        one = held([P, 1], F32, "one")

        for scales in (v2_table_scales, v_table_scales, b4_scales_in):
            nc.gpsimd.memset(scales[:].bitcast(I32), 0)
        nc.gpsimd.memset(one[:], 1.0)
        warm = held([P, 1], F32, "warm")
        nc.scalar.activation(out=warm[:], in_=one[:], func=ACT.Abs_reciprocal_sqrt)

        def load_words(i):
            src = tab_words[i] if i < 2 else tab2_words[0]
            nc.sync.dma_start(out=table_words[i][:], in_=src.rearrange("p t i -> p (t i)").bitcast(I32))

        def load_scales(scales, src, rows=range(4)):
            for r in rows:
                nc.sync.dma_start(out=scales[r:P:32, :].bitcast(I32), in_=src[0, r:16:4, :].bitcast(I32))

        def load_v_scales(n):
            for r in range(4):
                nc.sync.dma_start(
                    out=v_table_scales[4 + 4 * n + r : P : 32, :].bitcast(I32), in_=tab_scales[n, r:16:4, :].bitcast(I32)
                )

        def load_a(n, half):
            quarter = spare([P, PACK, PASS], "a_in", n)
            src = a[n * PASS : (n + 1) * PASS, half * PASS : (half + 1) * PASS]
            nc.sync.dma_start(out=quarter[:], in_=src.rearrange("(p j) c -> p j c", j=PACK))
            return quarter

        g_planes = gT.rearrange("(h q t s) n -> h t q s n", q=P // RUN, t=PACK, s=RUN)
        w_planes = w.rearrange("(h q t s) n -> h t q s n", q=P // RUN, t=PACK, s=RUN)

        def load_g(half):
            for t in range(PACK):
                nc.sync.dma_start(out=g_table[PACK * half + t][:], in_=g_planes[half, t])

        def load_w(half):
            w_in = held([P, PACK, N], F32, "w_in%d" % half, "table_words%d" % half)
            for t in range(PACK):
                nc.sync.dma_start(out=w_in[:, t, :], in_=w_planes[half, t])
            return w_in

        def negate(on_vector, dst, src):
            if on_vector:
                nc.vector.tensor_scalar(out=dst, in0=src, scalar1=-1.0, scalar2=None, op0=MULT)
            else:
                nc.scalar.activation(out=dst, in_=src, func=ACT.Copy, scale=-1.0)

        def round_a(n, quarter, planes_on_scalar):
            rounded = held([P, PACK, P, PACK], BF16, "a_rounded", "rounded%d" % n)
            dst = rounded[:].rearrange("p t (q s) j -> p t q j s", s=RUN)
            src = quarter[:].rearrange("p j (q t s) -> p t q j s", t=PACK, s=RUN)
            for t in range(PACK):
                negate(t >= planes_on_scalar, dst[:, t], src[:, t])
            return rounded

        def quantise_a(n, half, rounded, tag=None):
            cols = slice(half * PASS, (half + 1) * PASS)
            a_codes[n, half] = held([P, PASS], U32, "a_codes%d%d" % (n, half), tag)
            nc.vector.quantize_mx(
                out=a_codes[n, half][:].bitcast(FP8X4),
                scales=a_scale[n][:, cols],
                in_=rounded[:].rearrange("p t m j -> p (t m j)"),
            )

        w_rounded = held([P, 2 * N * PACK], BF16, "w_rounded")

        def round_w(c, half, w_in):
            w0 = (2 * c + half) * P * PACK
            dst = w_rounded[:, w0 : w0 + P * PACK].rearrange("p (c i t) -> p c t i", i=RUN, t=PACK)
            src = w_in[half][:, :, c * P : (c + 1) * P].rearrange("p t (c i) -> p c t i", i=RUN)
            negate(False, dst, src)

        def quantise_w(tag):
            w_codes = held([P, 2 * N], U32, "w_codes", tag)
            for c0, c1 in ((0, PASS), (PASS, 2 * N)):
                nc.vector.quantize_mx(
                    out=w_codes[:, c0:c1].bitcast(FP8X4),
                    scales=w_scale[:, c0:c1],
                    in_=w_rounded[:, PACK * c0 : PACK * c1],
                )
            return w_codes

        def deal_b4():
            nc.vector.tensor_copy(
                out=b4_codes[:].bitcast(I32).rearrange("p (h t q e) -> p h t q e", h=2, t=PACK, e=2),
                in_=b4_words_in[:].bitcast(I32).rearrange("p (h q t e) -> p h t q e", h=2, t=PACK, e=2),
            )
            nc.vector.tensor_copy(
                out=b4_scale[:].bitcast(I32).rearrange("p (h t q) -> p h t q", h=2, t=PACK),
                in_=b4_scales_in[:].bitcast(I32).rearrange("p (h q t) -> p h t q", h=2, t=PACK),
            )

        def entries(lst, first, count):
            return lst[:, first // LIST_ROWS : (first + count) // LIST_ROWS]

        def gather(dst, table, lst, first, count):
            nc.vector.tensor_copy(out=dst[:, first : first + count], in_=table.indirect(entries(lst, first, count)))

        banks = {}

        def displacement(half, first, squares):
            for off in range(0, squares[:].shape[2], BANK):
                bank = psum.tile([P, PACK, BANK], F32, name="bank", bufs=8)
                banks[half, first + off] = bank
                cols = slice(first + off, first + off + BANK)
                passes = [(t, n) for t in range(PACK) for n in range(3)]
                one_group = half == 1 or first + off < STEP
                if one_group:
                    passes = [(t, n) for n in ((0, 1, 2) if half == 0 else (2, 0, 1)) for t in range(PACK)]
                for t, n in passes:
                    m0 = half * PASS + t * P
                    with_a = n < 2
                    nc.tensor.matmul_mx(
                        out=bank[:, t, :],
                        lhsT=(
                            a_codes[n, half][:, t * P : (t + 1) * P].bitcast(FP8X4)
                            if with_a
                            else b4_codes[:, 2 * m0 : 2 * (m0 + P)].bitcast(FP4X4)
                        ),
                        lhsT_scale=(a_scale[n] if with_a else b4_scale)[:, m0 : m0 + P],
                        rhs=picked_words[n][:, cols].bitcast(FP8X4),
                        rhs_scale=v_scale[4 + 4 * n :, cols] if with_a else v2_scale[:, cols],
                        start=((t, n) == passes[0] if one_group else n == 0),
                        stop=((t, n) == passes[-1] if one_group else n == 2),
                    )
                nc.scalar.activation(out=squares[:, 0:PACK, off : off + BANK], in_=bank[:], func=ACT.Square)
            return squares

        def invert(half, squares, influence):
            planes = PASS // squares[:].shape[2]
            starts = [(t + (EARLY if half == 0 else 0)) % PACK for t in range(0, PACK, planes)]
            for two in range(0, len(starts), 2):
                pieces = [slice(t, t + planes) for t in starts[two : two + 2]]
                for piece in pieces:
                    nc.scalar.activation(
                        out=influence[:, piece, :], in_=squares[:, piece, :], func=ACT.Abs_reciprocal_sqrt, bias=one[:]
                    )
                for piece in pieces:
                    nc.scalar.activation(out=influence[:, piece, :], in_=influence[:, piece, :], func=ACT.Square)
            return influence

        def scalar_step(half, first, tile):
            return invert(half, displacement(half, first, tile), tile)

        def vector_step(half, first, influence, tag="weight", between=None):
            count = influence[:].shape[2]
            weight = held([P, PACK, count], F32, "weight", tag)[:] if half == 1 else influence[:, EARLY:, :]
            halves = (slice(0, count // 2), slice(count // 2, count))

            def gather_times_influence(t, part):
                nc.vector.tensor_tensor(
                    out=weight[:, t, part],
                    in0=g_table[PACK * half + t][:].indirect(entries(idx, first + part.start, part.stop - part.start)),
                    in1=influence[:, t, part],
                    op=MULT,
                )

            early = EARLY if half == 0 else 0
            for t in range(early, PACK - 1):
                gather_times_influence(t, slice(0, count))
            for part in halves:
                gather_times_influence(PACK - 1, part)
            for part in halves if early else ():
                nc.vector.tensor_tensor(
                    out=weight[:, 0:early, part],
                    in0=g_early[:, :, first + part.start : first + part.stop],
                    in1=influence[:, 0:early, part],
                    op=MULT,
                )
            h_rounded = ring.tile([P, count, PACK], BF16, name="h_rounded", bufs=2, align_bytes=64)
            for off in range(0, count, BANK):
                cols = slice(off, off + BANK)
                nc.vector.tensor_tensor(
                    out=h_rounded[:, cols, :].rearrange("p (c i) t -> p c t i", i=RUN),
                    in0=banks[half, first + off][:].rearrange("p t (c i) -> p c t i", i=RUN),
                    in1=weight[:, :, cols].rearrange("p t (c i) -> p c t i", i=RUN),
                    op=MULT,
                )
            if between is not None:
                between()
            for part in halves:
                cols = slice(first + part.start, first + part.stop)
                nc.vector.quantize_mx(
                    out=h_codes[half][:, cols].bitcast(FP8X4),
                    scales=h_scale[half][:, cols],
                    in_=h_rounded[:, part, :].rearrange("p n t -> p (n t)"),
                )

        out_rows = out.rearrange("(c p) j -> p c j", p=P)

        def forces(w_codes, first, count, blocks_on_vector):
            cols = slice(first, first + count)
            by_block = count > BANK or first + count == S
            if first == 0:
                stage = held([P, N // P, count], F32, "first_stage", "last_squares")
            elif count > BANK:
                stage = spare([P, N // P, count], "wide_stage", 0)
            else:
                stage = ring.tile([P, N // P, count], F32, name="stage", bufs=2)
            for c in range(N // P):
                acc = psum.tile([P, count], F32, name="bank", bufs=8)
                for half in range(2):
                    rows = slice((2 * c + half) * P, (2 * c + half + 1) * P)
                    nc.tensor.matmul_mx(
                        out=acc[:],
                        lhsT=w_codes[:, rows].bitcast(FP8X4),
                        lhsT_scale=w_scale[:, rows],
                        rhs=h_codes[half][:, cols].bitcast(FP8X4),
                        rhs_scale=h_scale[half][:, cols],
                        start=(half == 0),
                        stop=(half == 1),
                    )
                if c in blocks_on_vector:
                    nc.vector.tensor_copy(out=stage[:, c, :], in_=acc[:])
                else:
                    nc.scalar.copy(out=stage[:, c, :], in_=acc[:])
                if by_block:
                    nc.sync.dma_start(out=out_rows[:, c, cols], in_=stage[:, c, :])
            if not by_block:
                nc.sync.dma_start(out=out_rows[:, :, cols], in_=stage[:])

        nc.sync.dma_start(idx2[:], offs2)
        nc.sync.dma_start(out=b4_words_in[:].bitcast(I32), in_=b4_words[0].bitcast(I32))
        nc.sync.dma_start(idx[:], offs)
        load_scales(v2_table_scales, tab2_scales)
        load_words(0)
        load_v_scales(0)
        load_words(1)
        load_v_scales(1)
        a_00 = load_a(0, 0)
        load_scales(b4_scales_in, b4_scales, range(3))
        a_10 = load_a(1, 0)
        load_scales(b4_scales_in, b4_scales, range(3, 4))
        load_words(2)
        load_g(0)
        rounded_00 = round_a(0, a_00, PACK)
        rounded_10 = round_a(1, a_10, 3)
        a_01 = load_a(0, 1)
        a_11 = load_a(1, 1)
        load_g(1)

        quantise_a(0, 0, rounded_00)
        quantise_a(1, 0, rounded_10)
        gather(picked_words[2], table_words[2][:].bitcast(U32), idx2, 0, STEP)
        gather(picked_words[2], table_words[2][:].bitcast(U32), idx2, STEP, STEP)
        deal_b4()
        gather(v2_scale, v2_table_scales[:], idx2, 0, S)
        gather(picked_words[0], table_words[0][:].bitcast(U32), idx, 0, S)
        gather(v_scale, v_table_scales[:], idx, 0, S)
        gather(picked_words[1], table_words[1][:].bitcast(U32), idx, 0, S)

        w_in = [load_w(0), load_w(1)]

        first_influence = scalar_step(0, 0, held([P, PACK + EARLY, 2 * STEP], F32, "first_influence"))
        gather(picked_words[2], table_words[2][:].bitcast(U32), idx2, 2 * STEP, S - 2 * STEP)
        for t in range(EARLY):
            gather(g_early[:, t, :], g_table[t][:], idx, 0, S)
        squares = displacement(0, 2 * STEP, held([P, PACK, 2 * STEP], F32, "wide_squares"))
        rounded_01 = round_a(0, a_01, PACK)
        rounded_11 = round_a(1, a_11, 0)
        third_influence = invert(0, squares, spare([P, PACK + EARLY, 2 * STEP], "third_influence", 0))
        quantise_a(0, 1, rounded_01)
        quantise_a(1, 1, rounded_11)
        vector_step(0, 0, first_influence)
        vector_step(0, 2 * STEP, third_influence)

        fourth_influence = scalar_step(1, 0, held([P, PACK, STEP], F32, "fourth_influence", "first_influence"))
        fifth_influence = scalar_step(1, STEP, held([P, PACK, 2 * STEP], F32, "fifth_influence", "g_table0"))
        for half in range(2):
            for c in range(2):
                round_w(c, half, w_in)
        round_w(2, 0, w_in)
        squares = displacement(1, 3 * STEP, held([P, PACK, STEP], F32, "last_squares"))
        round_w(2, 1, w_in)
        last_influence = invert(1, squares, held([P, PACK, STEP], F32, "last_influence", "table_words0"))
        vector_step(1, 0, fourth_influence)
        made = []
        vector_step(1, STEP, fifth_influence, between=lambda: made.append(quantise_w("g_table0")))
        w_codes = made[0]
        forces(w_codes, 0, STEP, ())
        forces(w_codes, STEP, 2 * STEP, ())
        vector_step(1, 3 * STEP, last_influence)
        forces(w_codes, 3 * STEP, BANK, (2,))
        forces(w_codes, 3 * STEP + BANK, BANK, (0, 2))
